import numpy as np
import ml_dtypes


def mxq(x, axis, fmt="e4m3"):
    dtype, down = {"e4m3": (ml_dtypes.float8_e4m3fn, 7), "e5m2": (ml_dtypes.float8_e5m2, 14)}[fmt]
    v = np.moveaxis(np.asarray(x, np.float32).astype(ml_dtypes.bfloat16).astype(np.float64), axis, -1)
    blocks = v.reshape(v.shape[:-1] + (-1, 32))
    amax = np.abs(blocks).max(-1, keepdims=True)
    byte = np.maximum(np.where(amax > 0, np.frexp(amax)[1] - 1 + 127, 0) - down, 1)
    scale = np.exp2(byte - 127.0)
    codes = (blocks / scale).astype(np.float32).astype(dtype).astype(np.float64)
    return np.moveaxis((codes * scale).reshape(v.shape), -1, axis)


WIDE = False


def mx_kscale(k):
    if not WIDE:
        return np.ones(k)
    levels = np.array([10, -10, 5, -5, 0])
    if k % 512:
        return np.exp2(np.random.permutation(np.resize(levels, k // 32))).repeat(32)
    a = np.empty((k // 512, 16))
    for p in range(k // 512):
        a[p, :8] = np.random.permutation(np.resize(levels, 8))
        for g in range(8):
            far = levels[np.abs(levels - a[p, g]) >= 10]
            a[p, g + 8] = far[np.random.randint(len(far))]
    return np.exp2(a.ravel()).repeat(32)


def f64(x):
    return np.asarray(x).astype(np.float64)


def striped(idx):
    return np.tile(idx.reshape(-1, 16).T, (8, 1)).astype(np.uint16)


def unstriped(offs):
    return offs[:16].T.reshape(-1).astype(np.int64)


E2M1 = np.array([0.0, 0.5, 1.0, 1.5, 2.0, 3.0, 4.0, 6.0, -0.0, -0.5, -1.0, -1.5, -2.0, -3.0, -4.0, -6.0])


def pack_weight(w, fmt):
    k, n = w.shape
    w = f64(np.asarray(w, np.float32).astype(ml_dtypes.bfloat16)).reshape(k // 32, 32, n)
    amax = np.abs(w).max(1)
    if fmt == "e4m3":
        byte = np.frexp(amax)[1] - 1 + 127 - 7
    else:
        mant, ex = np.frexp(amax / 6.0)
        byte = np.where(mant > 0.5, ex, ex - 1) + 127
    byte = np.clip(np.where(amax > 0, byte, 1), 1, 254)
    scaled = (w * np.exp2(127.0 - byte)[:, None, :]).reshape(k, n).astype(np.float32)
    by_word = np.ascontiguousarray(scaled.reshape(k // 512, 128, 4, n).transpose(0, 1, 3, 2))
    if fmt == "e4m3":
        words = by_word.astype(ml_dtypes.float8_e4m3fn).view(np.uint8)
    else:
        c = by_word.astype(ml_dtypes.float4_e2m1fn).view(np.uint8) & 0xF
        words = (c[..., 0::2] | (c[..., 1::2] << 4)).reshape(k // 512, 128, 2 * n)
    return np.ascontiguousarray(words), np.ascontiguousarray(byte.astype(np.uint8).reshape(k // 512, 16, n))


def unpack_weight(words, scales, fmt):
    g, _, n = scales.shape
    words = np.ascontiguousarray(words).reshape(g, 128, n, -1)
    if fmt == "e4m3":
        vals = words.view(ml_dtypes.float8_e4m3fn).astype(np.float64)
    else:
        nib = np.empty((g, 128, n, 4), np.uint8)
        nib[..., 0::2] = words & 0xF
        nib[..., 1::2] = words >> 4
        vals = E2M1[nib]
    vals = vals * np.repeat(np.exp2(scales.astype(np.float64) - 127.0), 8, axis=1)[..., None]
    return vals.transpose(0, 1, 3, 2).reshape(g * 512, n)


def gelu(v):
    return 0.5 * v * (1.0 + np.tanh(np.sqrt(2.0 / np.pi) * (v + 0.044715 * v**3)))


def pack_table4(v):
    words, scales = pack_weight(v, "e2m1")
    g, t = words.shape[0] // 2, v.shape[1]
    words = words.reshape(g, 2, 128, t, 2).transpose(0, 2, 3, 1, 4)
    return np.concatenate([words.reshape(g, -1), scales.reshape(g, -1)], axis=1)


def unpack_table4(tab):
    g, t = tab.shape[0], tab.shape[1] // 544
    words = tab[:, :512 * t].reshape(g, 128, t, 2, 2).transpose(0, 3, 1, 2, 4).reshape(2 * g, 128, 2 * t)
    return unpack_weight(words, tab[:, 512 * t:].reshape(2 * g, 16, t), "e2m1")


K, T, S, H, N = 2048, 4096, 1024, 512, 768

def setup_inputs():
    n = np.random.standard_normal
    s = mx_kscale(K)[:, None]
    u = mx_kscale(H)[:, None]
    tab = pack_table4(n((K, T)) * s)
    offs = striped(np.random.permutation(T)[:S])
    enc = (n((K, H)) / np.sqrt(K) / s).astype(np.float32)
    b = (0.4 * n(H)).astype(np.float32)
    gain = (np.random.uniform(0.5, 1.5, H) * u[:, 0]).astype(np.float32)
    dec = (1.5 * n((H, N)) / np.sqrt(H) / u).astype(np.float32)
    tgt_words, tgt_scales = pack_weight(n((K, N)) / np.sqrt(K) / s, "e2m1")
    return {"tab": tab, "offs": offs, "enc": enc, "b": b, "gain": gain, "dec": dec,
            "tgt_words": tgt_words, "tgt_scales": tgt_scales}

def reference(tab, offs, enc, b, gain, dec, tgt_words, tgt_scales):
    v = unpack_table4(tab)[:, unstriped(offs)]
    tgt = unpack_weight(tgt_words, tgt_scales, "e2m1")
    encq = mxq(f64(enc), 0, "e4m3")
    decq = mxq(f64(dec), 0, "e4m3")
    a = encq.T @ v
    h = np.tanh(a + f64(b)[:, None]) * f64(gain)[:, None]
    hq = mxq(h, 0, "e4m3")
    d = decq.T @ hq
    y = tgt.T @ v
    return np.square(y - d)

@@ -1,0 +1,282 @@
+from contextlib import ExitStack
+
+import concourse.mybir as mybir
+
+K, T, S, H, N = 2048, 4096, 1024, 512, 768
+FLOPS = 2 * S * (K * H + K * N + H * N)
+
+F32 = mybir.dt.float32
+BF16 = mybir.dt.bfloat16
+I32 = mybir.dt.int32
+U32 = mybir.dt.uint32
+U16 = mybir.dt.uint16
+U8 = mybir.dt.uint8
+FP8X4 = mybir.dt.float8_e4m3fn_x4
+FP4X4 = mybir.dt.float4_e2m1fn_x4
+ACT = mybir.ActivationFunctionType
+ALU = mybir.AluOpType
+
+P = 128
+PACK = 4
+PASSES = K // (P * PACK)
+PAIRS = PASSES // 2
+HALF = 512
+HALVES = S // HALF
+N_TILES = N // P
+WORD_BYTES = 512 * T
+ENC_VECTOR_SHARE = (128, 128, 80, 80)
+DEC_CHUNK = 256
+H_CHUNK = 256
+
+
+def tile_list_alarm_anomaly_maps_kernel(tc, tab, offs, enc, b, gain, dec, tgt_words, tgt_scales, out):
+    nc = tc.nc
+    with ExitStack() as ctx:
+        keep = ctx.enter_context(tc.tile_pool(name="keep", bufs=1))
+        ring = ctx.enter_context(tc.tile_pool(name="ring", bufs=4))
+        psum = ctx.enter_context(tc.psum_pool(name="psum", bufs=1))
+
+        def held(name, shape, dtype):
+            return keep.tile(shape, dtype, name=name, align_bytes=64)
+
+        def bank(i):
+            return psum.tile([P, HALF], F32, name=f"bank{i}", tag=f"bank{i}")
+
+        offsets = keep.tile([P, S // 16], U16, name="offsets")
+        nc.sync.dma_start(offsets[:], offs)
+
+        scale_rows = held("scale_rows", [P, T // 4], I32)
+        tgt_sc = held("tgt_sc", [P, PASSES, N // 4], I32)
+        moved_sc = held("moved_sc", [P, PASSES - 1, S // 4], I32)
+        warm = held("warm", [P, 8], F32)
+        nc.vector.memset(scale_rows[:], 0)
+        nc.vector.memset(tgt_sc[:], 0)
+        nc.vector.memset(moved_sc[:], 0)
+        nc.vector.memset(warm[:], 0.0)
+
+        b_sb = held("b_sb", [P, PACK], F32)
+        nc.sync.dma_start(b_sb[:], b.rearrange("(p t) -> p t", t=PACK))
+        for m, queue in ((0, nc.scalar), (1, nc.sync)):
+            rows = tab[m, WORD_BYTES:].bitcast(I32).rearrange("(h q r t) -> r q h t", h=2, q=4, r=4)
+            for r in range(4):
+                queue.dma_start(scale_rows[4 * m + r : P : 16, :], rows[r])
+
+        words = [held(f"words{m}", [P, T], I32) for m in range(PAIRS)]
+        tgt_w = [held(f"tgt_w{m}", [P, 2, 2 * N // 4], I32) for m in range(PAIRS)]
+        enc_raw = [held(f"enc_raw{a}", [P, PACK, H], F32) for a in range(PASSES)]
+        dec_raw = held("dec_raw", [P, PACK, N], F32)
+        gain_sb = held("gain_sb", [P, PACK], F32)
+
+        def load_words(m):
+            nc.sync.dma_start(words[m][:], tab[m, :WORD_BYTES].bitcast(I32).rearrange("(p t) -> p t", p=P))
+
+        def load_tgt(m):
+            nc.sync.dma_start(tgt_w[m][:], tgt_words[2 * m : 2 * m + 2].bitcast(I32).rearrange("a p c -> p a c"))
+
+        load_words(0)
+        for q in range(4):
+            nc.scalar.dma_start(
+                tgt_sc[32 * q : 32 * q + 4, :, :],
+                tgt_scales[:, 4 * q : 4 * q + 4, :].bitcast(I32).rearrange("a r c -> r a c"),
+            )
+        nc.scalar.activation(warm[:], warm[:], ACT.Tanh)
+        load_tgt(0)
+        load_words(1)
+        load_tgt(1)
+        for a in range(PASSES):
+            nc.sync.dma_start(enc_raw[a][:], enc[512 * a : 512 * (a + 1), :].rearrange("(p j) c -> p j c", j=PACK))
+            if a == 1:
+                nc.sync.dma_start(gain_sb[:], gain.rearrange("(p t) -> p t", t=PACK))
+        nc.sync.dma_start(dec_raw[:], dec.rearrange("(p j) c -> p j c", j=PACK))
+
+        picked_sc = held("picked_sc", [P, S // 4], I32)
+        nc.vector.tensor_copy(picked_sc[:].bitcast(U8), scale_rows[:].bitcast(U8).indirect(offsets[:]))
+        v_scales = [picked_sc[:].bitcast(U8)]
+        for a in range(1, PASSES):
+            shift = 16 * (a % 2) + 4 * (a // 2)
+            n_rows = min(112, P - shift)
+            nc.scalar.dma_start(moved_sc[0:n_rows, a - 1, :], picked_sc[shift : shift + n_rows, :])
+            v_scales.append(moved_sc[:, a - 1, :].bitcast(U8))
+
+        v_words = {}
+
+        def gather(m, u):
+            picked = held(f"picked{m}{u}", [P, HALF], I32)
+            cols = slice(u * HALF // 16, (u + 1) * HALF // 16)
+            nc.vector.tensor_copy(picked[:].bitcast(U32), words[m][:].bitcast(U32).indirect(offsets[:, cols]))
+            parted = held(f"parted{m}{u}", [P, 2, HALF], U16)
+            nc.vector.tensor_copy(parted[:], picked[:].bitcast(U16).rearrange("p (s h) -> p h s", h=2))
+            for h in range(2):
+                v_words[2 * m + h, u] = parted[:, h, :].bitcast(FP4X4)
+
+        def v_operand(a, u):
+            return dict(rhs=v_words[a, u], rhs_scale=v_scales[a][:, u * HALF : (u + 1) * HALF])
+
+        def y_pass(acc, n, u, a):
+            nc.tensor.matmul_mx(
+                out=acc[:],
+                lhsT=tgt_w[a // 2][:, a % 2, 64 * n : 64 * (n + 1)].bitcast(FP4X4),
+                lhsT_scale=tgt_sc[:, a, 32 * n : 32 * (n + 1)].bitcast(U8),
+                start=(a == 0),
+                stop=(a == PASSES - 1),
+                **v_operand(a, u),
+            )
+
+        y_sb = {}
+
+        def keep_y(acc, n, u):
+            y_sb[n, u] = held(f"y{n}{u}", [P, HALF], F32)
+            nc.scalar.copy(y_sb[n, u][:], acc[:])
+
+        early = [(n, 0) for n in range(N_TILES)] + [(0, 1), (1, 1)]
+        acc = [bank(i) for i in range(8)]
+        for u in range(HALVES):
+            gather(0, u)
+            for a in (0, 1):
+                for i, (n, uu) in enumerate(early):
+                    if uu == u:
+                        y_pass(acc[i], n, u, a)
+        for u in range(HALVES):
+            gather(1, u)
+            for i, (n, uu) in enumerate(early):
+                if uu == u:
+                    for a in (2, 3):
+                        y_pass(acc[i], n, u, a)
+                    keep_y(acc[i], n, u)
+
+        enc_q = []
+        a_acc = {}
+        th = [held(f"th{u}", [P, PACK, HALF], F32) for u in range(HALVES)]
+
+        def a_pass(a, u, t):
+            codes, scales = enc_q[a]
+            nc.tensor.matmul_mx(
+                out=a_acc[u, t][:],
+                lhsT=codes[:, P * t : P * (t + 1)].bitcast(FP8X4),
+                lhsT_scale=scales[:, P * t : P * (t + 1)],
+                start=(a == 0),
+                stop=(a == PASSES - 1),
+                **v_operand(a, u),
+            )
+
+        def tanh(u, c):
+            cols = slice(c * H_CHUNK, (c + 1) * H_CHUNK)
+            for t in range(PACK):
+                nc.scalar.activation(th[u][:, t, cols], a_acc[u, t][:, cols], ACT.Tanh, bias=b_sb[:, t : t + 1])
+
+        beside_loads = [(0, t) for t in range(PACK)] + [(1, 0), (1, 1)]
+        for i, key in enumerate(beside_loads):
+            a_acc[key] = bank(i)
+        for a in range(PASSES):
+            grouped = held(f"enc_bf{a}", [P, PACK * H], BF16)
+            dst = grouped[:].rearrange("p (t m j) -> p m t j", t=PACK, j=PACK)
+            src = enc_raw[a][:].rearrange("p j (m t) -> p m t j", t=PACK)
+            cut = ENC_VECTOR_SHARE[a]
+            nc.vector.tensor_copy(dst[:, :cut], src[:, :cut])
+            if cut < P:
+                nc.scalar.copy(dst[:, cut:], src[:, cut:])
+            codes = held(f"enc_codes{a}", [P, H], U32)
+            scales = held(f"enc_scales{a}", [P, H], U8)
+            nc.vector.quantize_mx(out=codes[:].bitcast(FP8X4), scales=scales[:], in_=grouped[:])
+            enc_q.append((codes, scales))
+            for u, t in beside_loads:
+                a_pass(a, u, t)
+        tanh(0, 0)
+        tanh(0, 1)
+        for t in (2, 3):
+            a_acc[1, t] = bank(t - 2)
+            for a in range(PASSES):
+                a_pass(a, 1, t)
+
+        dec_bf = held("dec_bf", [P, PACK * N], BF16)
+        dec_codes = held("dec_codes", [P, N], U32)
+        dec_scales = held("dec_scales", [P, N], U8)
+
+        def cast_dec(c):
+            cols = slice(c * DEC_CHUNK, (c + 1) * DEC_CHUNK)
+            wide = slice(c * DEC_CHUNK * PACK, (c + 1) * DEC_CHUNK * PACK)
+            dst = dec_bf[:, wide].rearrange("p (c i t) -> p c t i", i=4, t=PACK)
+            src = dec_raw[:, :, cols].rearrange("p t (c i) -> p c t i", i=4)
+            if c == 0:
+                nc.vector.tensor_copy(dst, src)
+            else:
+                nc.scalar.copy(dst, src)
+
+        def quantize_dec(c):
+            cols = slice(c * DEC_CHUNK, (c + 1) * DEC_CHUNK)
+            wide = slice(c * DEC_CHUNK * PACK, (c + 1) * DEC_CHUNK * PACK)
+            nc.vector.quantize_mx(out=dec_codes[:, cols].bitcast(FP8X4), scales=dec_scales[:, cols], in_=dec_bf[:, wide])
+
+        h_codes = [held(f"h_codes{u}", [P, HALF], U32) for u in range(HALVES)]
+        h_scales = [held(f"h_scales{u}", [P, HALF], U8) for u in range(HALVES)]
+
+        h_bf = [held(f"h_bf{u}", [P, PACK * HALF], BF16) for u in range(HALVES)]
+        gains = gain_sb[:].rearrange("p (c t i) -> p c t i", c=1, i=1).to_broadcast([P, H_CHUNK // 4, PACK, 4])
+
+        def scale_h(u, c):
+            cols = slice(c * H_CHUNK, (c + 1) * H_CHUNK)
+            wide = slice(c * H_CHUNK * PACK, (c + 1) * H_CHUNK * PACK)
+            nc.vector.tensor_tensor(
+                h_bf[u][:, wide].rearrange("p (c i t) -> p c t i", i=4, t=PACK),
+                th[u][:, :, cols].rearrange("p t (c i) -> p c t i", i=4),
+                gains,
+                ALU.mult,
+            )
+
+        def quantize_h(u, c):
+            cols = slice(c * H_CHUNK, (c + 1) * H_CHUNK)
+            wide = slice(c * H_CHUNK * PACK, (c + 1) * H_CHUNK * PACK)
+            nc.vector.quantize_mx(out=h_codes[u][:, cols].bitcast(FP8X4), scales=h_scales[u][:, cols], in_=h_bf[u][:, wide])
+
+        def finish(n, u, i):
+            d = bank(i)
+            nc.tensor.matmul_mx(
+                out=d[:],
+                lhsT=dec_codes[:, P * n : P * (n + 1)].bitcast(FP8X4),
+                lhsT_scale=dec_scales[:, P * n : P * (n + 1)],
+                rhs=h_codes[u][:].bitcast(FP8X4),
+                rhs_scale=h_scales[u][:],
+                start=True,
+                stop=True,
+            )
+            diff = ring.tile([P, HALF], F32, name="diff")
+            nc.vector.tensor_tensor(diff[:], y_sb[n, u][:], d[:], ALU.subtract)
+            res = ring.tile([P, HALF], F32, name="res")
+            nc.scalar.activation(res[:], diff[:], ACT.Square)
+            nc.sync.dma_start(out[P * n : P * (n + 1), u * HALF : (u + 1) * HALF], res[:])
+
+        def late_y(n, i):
+            acc_late = bank(i)
+            for a in range(PASSES):
+                y_pass(acc_late, n, 1, a)
+            keep_y(acc_late, n, 1)
+
+        scale_h(0, 0)
+        cast_dec(0)
+        scale_h(0, 1)
+        quantize_h(0, 0)
+        quantize_dec(0)
+        quantize_h(0, 1)
+        cast_dec(1)
+        tanh(1, 0)
+        tanh(1, 1)
+        finish(0, 0, 6)
+        finish(1, 0, 7)
+        quantize_dec(1)
+        cast_dec(2)
+        scale_h(1, 0)
+        finish(2, 0, 6)
+        scale_h(1, 1)
+        finish(3, 0, 7)
+        quantize_dec(2)
+        quantize_h(1, 0)
+        quantize_h(1, 1)
+        late_y(2, 2)
+        finish(4, 0, 6)
+        late_y(3, 3)
+        finish(5, 0, 7)
+        late_y(4, 4)
+        finish(0, 1, 0)
+        late_y(5, 5)
+        for n in range(1, N_TILES):
+            finish(n, 1, (0, 1, 6, 7, 2, 3)[n])

@@ -24,20 +24,23 @@ HALF = 512
 HALVES = S // HALF
 N_TILES = N // P
 WORD_BYTES = 512 * T
-ENC_VECTOR_SHARE = (128, 128, 80, 80)
+ENC_SCALAR_SHARE = ((32,), (0,), (72,), (16, 24))
+Y_SLOT = {(1, 1): 'enc_raw31', (3, 1): 'enc_raw20', (0, 1): 'enc_raw00', (2, 1): 'enc_raw30'}
+ENC_PIECES = (1, 1, 1, 2)
 DEC_CHUNK = 256
 H_CHUNK = 256
+TILE_WORDS = 2 * P // 4
+EARLY_TILES = 4
 
 
 def tile_list_alarm_anomaly_maps_kernel(tc, tab, offs, enc, b, gain, dec, tgt_words, tgt_scales, out):
     nc = tc.nc
     with ExitStack() as ctx:
         keep = ctx.enter_context(tc.tile_pool(name="keep", bufs=1))
-        ring = ctx.enter_context(tc.tile_pool(name="ring", bufs=4))
         psum = ctx.enter_context(tc.psum_pool(name="psum", bufs=1))
 
-        def held(name, shape, dtype):
-            return keep.tile(shape, dtype, name=name, align_bytes=64)
+        def held(name, shape, dtype, tag=None):
+            return keep.tile(shape, dtype, name=name, tag=tag or name, align_bytes=64)
 
         def bank(i):
             return psum.tile([P, HALF], F32, name=f"bank{i}", tag=f"bank{i}")
@@ -47,61 +50,70 @@ def tile_list_alarm_anomaly_maps_kernel(tc, tab, offs, enc, b, gain, dec, tgt_wo
 
         scale_rows = held("scale_rows", [P, T // 4], I32)
         tgt_sc = held("tgt_sc", [P, PASSES, N // 4], I32)
-        moved_sc = held("moved_sc", [P, PASSES - 1, S // 4], I32)
+        v_sc = held("v_sc", [P, PASSES, S // 4], I32)
         warm = held("warm", [P, 8], F32)
-        nc.vector.memset(scale_rows[:], 0)
         nc.vector.memset(tgt_sc[:], 0)
-        nc.vector.memset(moved_sc[:], 0)
+        nc.vector.memset(scale_rows[0:32, :], 0)
+        nc.vector.memset(scale_rows[96:P, :], 0)
+        nc.vector.memset(v_sc[:], 0)
         nc.vector.memset(warm[:], 0.0)
 
-        b_sb = held("b_sb", [P, PACK], F32)
-        nc.sync.dma_start(b_sb[:], b.rearrange("(p t) -> p t", t=PACK))
-        for m, queue in ((0, nc.scalar), (1, nc.sync)):
-            rows = tab[m, WORD_BYTES:].bitcast(I32).rearrange("(h q r t) -> r q h t", h=2, q=4, r=4)
-            for r in range(4):
-                queue.dma_start(scale_rows[4 * m + r : P : 16, :], rows[r])
-
         words = [held(f"words{m}", [P, T], I32) for m in range(PAIRS)]
-        tgt_w = [held(f"tgt_w{m}", [P, 2, 2 * N // 4], I32) for m in range(PAIRS)]
-        enc_raw = [held(f"enc_raw{a}", [P, PACK, H], F32) for a in range(PASSES)]
+        tgt_w = [held(f"tgt_w{m}", [P, 2, EARLY_TILES * TILE_WORDS], I32) for m in range(PAIRS)]
+        tgt_last = held("tgt_last", [P, PASSES, (N_TILES - EARLY_TILES) * TILE_WORDS], I32)
+        enc_raw = {
+            (a, c): held(f"enc_raw{a}{c}", [P, PACK, H // ENC_PIECES[a]], F32)
+            for a in range(PASSES)
+            for c in range(ENC_PIECES[a])
+        }
         dec_raw = held("dec_raw", [P, PACK, N], F32)
+        b_sb = held("b_sb", [P, PACK], F32)
         gain_sb = held("gain_sb", [P, PACK], F32)
+        tgt_rows = tgt_words.bitcast(I32).rearrange("a p c -> p a c")
 
         def load_words(m):
             nc.sync.dma_start(words[m][:], tab[m, :WORD_BYTES].bitcast(I32).rearrange("(p t) -> p t", p=P))
 
         def load_tgt(m):
-            nc.sync.dma_start(tgt_w[m][:], tgt_words[2 * m : 2 * m + 2].bitcast(I32).rearrange("a p c -> p a c"))
+            nc.sync.dma_start(tgt_w[m][:], tgt_rows[:, 2 * m : 2 * m + 2, : EARLY_TILES * TILE_WORDS])
 
-        load_words(0)
+        for m in range(PAIRS):
+            rows = tab[m, WORD_BYTES:].bitcast(I32).rearrange("(h q t) -> q h t", h=2, q=16)
+            nc.sync.dma_start(scale_rows[32 + m : 96 : 2, :], rows)
         for q in range(4):
-            nc.scalar.dma_start(
+            nc.sync.dma_start(
                 tgt_sc[32 * q : 32 * q + 4, :, :],
                 tgt_scales[:, 4 * q : 4 * q + 4, :].bitcast(I32).rearrange("a r c -> r a c"),
             )
+        load_words(0)
         nc.scalar.activation(warm[:], warm[:], ACT.Tanh)
-        load_tgt(0)
-        load_words(1)
-        load_tgt(1)
-        for a in range(PASSES):
-            nc.sync.dma_start(enc_raw[a][:], enc[512 * a : 512 * (a + 1), :].rearrange("(p j) c -> p j c", j=PACK))
-            if a == 1:
-                nc.sync.dma_start(gain_sb[:], gain.rearrange("(p t) -> p t", t=PACK))
-        nc.sync.dma_start(dec_raw[:], dec.rearrange("(p j) c -> p j c", j=PACK))
 
         picked_sc = held("picked_sc", [P, S // 4], I32)
         nc.vector.tensor_copy(picked_sc[:].bitcast(U8), scale_rows[:].bitcast(U8).indirect(offsets[:]))
-        v_scales = [picked_sc[:].bitcast(U8)]
-        for a in range(1, PASSES):
-            shift = 16 * (a % 2) + 4 * (a // 2)
-            n_rows = min(112, P - shift)
-            nc.scalar.dma_start(moved_sc[0:n_rows, a - 1, :], picked_sc[shift : shift + n_rows, :])
-            v_scales.append(moved_sc[:, a - 1, :].bitcast(U8))
+        for q in range(4):
+            nc.sync.dma_start(v_sc[32 * q : 32 * q + 4, :, :], picked_sc[32 + 16 * q : 48 + 16 * q, :])
+        v_scales = [v_sc[:, 2 * (a % 2) + a // 2, :].bitcast(U8) for a in range(PASSES)]
+
+        load_tgt(0)
+        load_words(1)
+        nc.gpsimd.dma_start(b_sb[:], b.rearrange("(p t) -> p t", t=PACK))
+        nc.gpsimd.dma_start(gain_sb[:], gain.rearrange("(p t) -> p t", t=PACK))
+        load_tgt(1)
+        for a in range(PASSES):
+            rows = enc[512 * a : 512 * (a + 1), :].rearrange("(p j) c -> p j c", j=PACK)
+            width = H // ENC_PIECES[a]
+            for c in range(ENC_PIECES[a]):
+                nc.sync.dma_start(enc_raw[a, c][:], rows[:, :, c * width : (c + 1) * width])
+        dec_rows = dec.rearrange("(p j) c -> p j c", j=PACK)
+        for c in range(0, N, DEC_CHUNK):
+            nc.sync.dma_start(dec_raw[:, :, c : c + DEC_CHUNK], dec_rows[:, :, c : c + DEC_CHUNK])
+            if c == 1 * DEC_CHUNK:
+                nc.sync.dma_start(tgt_last[:], tgt_rows[:, :, EARLY_TILES * TILE_WORDS :])
 
         v_words = {}
 
         def gather(m, u):
-            picked = held(f"picked{m}{u}", [P, HALF], I32)
+            picked = held("picked", [P, HALF], I32)
             cols = slice(u * HALF // 16, (u + 1) * HALF // 16)
             nc.vector.tensor_copy(picked[:].bitcast(U32), words[m][:].bitcast(U32).indirect(offsets[:, cols]))
             parted = held(f"parted{m}{u}", [P, 2, HALF], U16)
@@ -113,9 +125,13 @@ def tile_list_alarm_anomaly_maps_kernel(tc, tab, offs, enc, b, gain, dec, tgt_wo
             return dict(rhs=v_words[a, u], rhs_scale=v_scales[a][:, u * HALF : (u + 1) * HALF])
 
         def y_pass(acc, n, u, a):
+            if n < EARLY_TILES:
+                codes = tgt_w[a // 2][:, a % 2, TILE_WORDS * n : TILE_WORDS * (n + 1)]
+            else:
+                codes = tgt_last[:, a, TILE_WORDS * (n - EARLY_TILES) : TILE_WORDS * (n - EARLY_TILES + 1)]
             nc.tensor.matmul_mx(
                 out=acc[:],
-                lhsT=tgt_w[a // 2][:, a % 2, 64 * n : 64 * (n + 1)].bitcast(FP4X4),
+                lhsT=codes.bitcast(FP4X4),
                 lhsT_scale=tgt_sc[:, a, 32 * n : 32 * (n + 1)].bitcast(U8),
                 start=(a == 0),
                 stop=(a == PASSES - 1),
@@ -125,26 +141,55 @@ def tile_list_alarm_anomaly_maps_kernel(tc, tab, offs, enc, b, gain, dec, tgt_wo
         y_sb = {}
 
         def keep_y(acc, n, u):
-            y_sb[n, u] = held(f"y{n}{u}", [P, HALF], F32)
+            y_sb[n, u] = held(f"y{n}{u}", [P, HALF], F32, tag=Y_SLOT.get((n, u)))
             nc.scalar.copy(y_sb[n, u][:], acc[:])
 
-        early = [(n, 0) for n in range(N_TILES)] + [(0, 1), (1, 1)]
-        acc = [bank(i) for i in range(8)]
+        y_acc = {}
+
+        def late_y(n, u, i):
+            y_acc[n, u] = bank(i)
+            for a in range(PASSES):
+                y_pass(y_acc[n, u], n, u, a)
+
+        def park(n, u):
+            keep_y(y_acc[n, u] if n >= EARLY_TILES else accs[EARLY_TILES + n], n, u)
+
+        first = [(n, 0) for n in range(EARLY_TILES)] + [(n, 1) for n in range(8 - EARLY_TILES)]
+        accs = [bank(i) for i in range(8)]
         for u in range(HALVES):
             gather(0, u)
             for a in (0, 1):
-                for i, (n, uu) in enumerate(early):
+                for i, (n, uu) in enumerate(first):
                     if uu == u:
-                        y_pass(acc[i], n, u, a)
+                        y_pass(accs[i], n, u, a)
         for u in range(HALVES):
             gather(1, u)
-            for i, (n, uu) in enumerate(early):
-                if uu == u:
-                    for a in (2, 3):
-                        y_pass(acc[i], n, u, a)
-                    keep_y(acc[i], n, u)
 
         enc_q = []
+        for a in range(PASSES):
+            grouped = held(f"enc_bf{a}", [P, PACK * H], BF16)
+            dst = grouped[:].rearrange("p (t m j) -> p m t j", t=PACK, j=PACK)
+            width = P // ENC_PIECES[a]
+            for c in range(ENC_PIECES[a]):
+                src = enc_raw[a, c][:].rearrange("p j (m t) -> p m t j", t=PACK)
+                cut = width - ENC_SCALAR_SHARE[a][c]
+                if cut > 0:
+                    nc.vector.tensor_copy(dst[:, c * width : c * width + cut], src[:, :cut])
+                if cut < width:
+                    nc.scalar.copy(dst[:, c * width + cut : (c + 1) * width], src[:, cut:])
+            codes = held(f"enc_codes{a}", [P, H], U32)
+            scales = held(f"enc_scales{a}", [P, H], U8)
+            nc.vector.quantize_mx(out=codes[:].bitcast(FP8X4), scales=scales[:], in_=grouped[:])
+            enc_q.append((codes, scales))
+
+        for u in range(HALVES):
+            for i, (n, uu) in enumerate(first):
+                if uu == u:
+                    for a in (2, 3):
+                        y_pass(accs[i], n, u, a)
+                    if u == 0:
+                        keep_y(accs[i], n, u)
+
         a_acc = {}
         th = [held(f"th{u}", [P, PACK, HALF], F32) for u in range(HALVES)]
 
@@ -159,48 +204,39 @@ def tile_list_alarm_anomaly_maps_kernel(tc, tab, offs, enc, b, gain, dec, tgt_wo
                 **v_operand(a, u),
             )
 
-        def tanh(u, c):
-            cols = slice(c * H_CHUNK, (c + 1) * H_CHUNK)
-            for t in range(PACK):
-                nc.scalar.activation(th[u][:, t, cols], a_acc[u, t][:, cols], ACT.Tanh, bias=b_sb[:, t : t + 1])
+        def tanh(u, t, cols):
+            nc.scalar.activation(th[u][:, t, cols], a_acc[u, t][:, cols], ACT.Tanh, bias=b_sb[:, t : t + 1])
 
-        beside_loads = [(0, t) for t in range(PACK)] + [(1, 0), (1, 1)]
-        for i, key in enumerate(beside_loads):
-            a_acc[key] = bank(i)
+        chunks = [slice(c * H_CHUNK, (c + 1) * H_CHUNK) for c in range(HALF // H_CHUNK)]
+        for t in range(PACK):
+            a_acc[0, t] = bank(t)
         for a in range(PASSES):
-            grouped = held(f"enc_bf{a}", [P, PACK * H], BF16)
-            dst = grouped[:].rearrange("p (t m j) -> p m t j", t=PACK, j=PACK)
-            src = enc_raw[a][:].rearrange("p j (m t) -> p m t j", t=PACK)
-            cut = ENC_VECTOR_SHARE[a]
-            nc.vector.tensor_copy(dst[:, :cut], src[:, :cut])
-            if cut < P:
-                nc.scalar.copy(dst[:, cut:], src[:, cut:])
-            codes = held(f"enc_codes{a}", [P, H], U32)
-            scales = held(f"enc_scales{a}", [P, H], U8)
-            nc.vector.quantize_mx(out=codes[:].bitcast(FP8X4), scales=scales[:], in_=grouped[:])
-            enc_q.append((codes, scales))
-            for u, t in beside_loads:
-                a_pass(a, u, t)
-        tanh(0, 0)
-        tanh(0, 1)
-        for t in (2, 3):
-            a_acc[1, t] = bank(t - 2)
+            for t in range(PACK):
+                a_pass(a, 0, t)
+        for cols in chunks:
+            for t in range(PACK):
+                tanh(0, t, cols)
+
+        def encode(t, i):
+            a_acc[1, t] = bank(i)
             for a in range(PASSES):
                 a_pass(a, 1, t)
+
+        def tanh_late(t):
+            for cols in chunks if t == PACK - 1 else [slice(0, HALF)]:
+                tanh(1, t, cols)
 
         dec_bf = held("dec_bf", [P, PACK * N], BF16)
         dec_codes = held("dec_codes", [P, N], U32)
         dec_scales = held("dec_scales", [P, N], U8)
 
-        def cast_dec(c):
+        def cast_dec(c, copy):
             cols = slice(c * DEC_CHUNK, (c + 1) * DEC_CHUNK)
             wide = slice(c * DEC_CHUNK * PACK, (c + 1) * DEC_CHUNK * PACK)
-            dst = dec_bf[:, wide].rearrange("p (c i t) -> p c t i", i=4, t=PACK)
-            src = dec_raw[:, :, cols].rearrange("p t (c i) -> p c t i", i=4)
-            if c == 0:
-                nc.vector.tensor_copy(dst, src)
-            else:
-                nc.scalar.copy(dst, src)
+            copy(
+                dec_bf[:, wide].rearrange("p (c i t) -> p c t i", i=4, t=PACK),
+                dec_raw[:, :, cols].rearrange("p t (c i) -> p c t i", i=4),
+            )
 
         def quantize_dec(c):
             cols = slice(c * DEC_CHUNK, (c + 1) * DEC_CHUNK)
@@ -209,27 +245,29 @@ def tile_list_alarm_anomaly_maps_kernel(tc, tab, offs, enc, b, gain, dec, tgt_wo
 
         h_codes = [held(f"h_codes{u}", [P, HALF], U32) for u in range(HALVES)]
         h_scales = [held(f"h_scales{u}", [P, HALF], U8) for u in range(HALVES)]
-
         h_bf = [held(f"h_bf{u}", [P, PACK * HALF], BF16) for u in range(HALVES)]
         gains = gain_sb[:].rearrange("p (c t i) -> p c t i", c=1, i=1).to_broadcast([P, H_CHUNK // 4, PACK, 4])
 
         def scale_h(u, c):
-            cols = slice(c * H_CHUNK, (c + 1) * H_CHUNK)
             wide = slice(c * H_CHUNK * PACK, (c + 1) * H_CHUNK * PACK)
             nc.vector.tensor_tensor(
                 h_bf[u][:, wide].rearrange("p (c i t) -> p c t i", i=4, t=PACK),
-                th[u][:, :, cols].rearrange("p t (c i) -> p c t i", i=4),
+                th[u][:, :, chunks[c]].rearrange("p t (c i) -> p c t i", i=4),
                 gains,
                 ALU.mult,
             )
 
         def quantize_h(u, c):
-            cols = slice(c * H_CHUNK, (c + 1) * H_CHUNK)
             wide = slice(c * H_CHUNK * PACK, (c + 1) * H_CHUNK * PACK)
-            nc.vector.quantize_mx(out=h_codes[u][:, cols].bitcast(FP8X4), scales=h_scales[u][:, cols], in_=h_bf[u][:, wide])
+            nc.vector.quantize_mx(
+                out=h_codes[u][:, chunks[c]].bitcast(FP8X4), scales=h_scales[u][:, chunks[c]], in_=h_bf[u][:, wide]
+            )
 
-        def finish(n, u, i):
-            d = bank(i)
+        d_acc = {}
+        diffs = {}
+
+        def decode(n, u, i):
+            d = d_acc[n, u] = bank(i)
             nc.tensor.matmul_mx(
                 out=d[:],
                 lhsT=dec_codes[:, P * n : P * (n + 1)].bitcast(FP8X4),
@@ -239,44 +277,92 @@ def tile_list_alarm_anomaly_maps_kernel(tc, tab, offs, enc, b, gain, dec, tgt_wo
                 start=True,
                 stop=True,
             )
-            diff = ring.tile([P, HALF], F32, name="diff")
-            nc.vector.tensor_tensor(diff[:], y_sb[n, u][:], d[:], ALU.subtract)
-            res = ring.tile([P, HALF], F32, name="res")
-            nc.scalar.activation(res[:], diff[:], ACT.Square)
-            nc.sync.dma_start(out[P * n : P * (n + 1), u * HALF : (u + 1) * HALF], res[:])
 
-        def late_y(n, i):
-            acc_late = bank(i)
-            for a in range(PASSES):
-                y_pass(acc_late, n, 1, a)
-            keep_y(acc_late, n, 1)
+        def subtract(n, u, pieces=1):
+            diffs[n, u] = held(f"diff{n}{u}", [P, HALF], F32)
+            width = HALF // pieces
+            for c in range(0, HALF, width):
+                cols = slice(c, c + width)
+                nc.vector.tensor_tensor(diffs[n, u][:, cols], y_sb[n, u][:, cols], d_acc[n, u][:, cols], ALU.subtract)
 
+        def square(n, u, on_gpsimd=False, pieces=1):
+            diff, res = diffs[n, u], y_sb[n, u]
+            width = HALF // pieces
+            for c in range(0, HALF, width):
+                cols = slice(c, c + width)
+                if on_gpsimd:
+                    nc.gpsimd.tensor_tensor(res[:, cols], diff[:, cols], diff[:, cols], ALU.mult)
+                else:
+                    nc.scalar.activation(res[:, cols], diff[:, cols], ACT.Square)
+                nc.sync.dma_start(out[P * n : P * (n + 1), u * HALF + c : u * HALF + c + width], res[:, cols])
+
+        encode(1, 1)
+        park(2, 1)
         scale_h(0, 0)
-        cast_dec(0)
         scale_h(0, 1)
         quantize_h(0, 0)
-        quantize_dec(0)
+        cast_dec(0, nc.vector.tensor_copy)
         quantize_h(0, 1)
-        cast_dec(1)
-        tanh(1, 0)
-        tanh(1, 1)
-        finish(0, 0, 6)
-        finish(1, 0, 7)
+        encode(0, 0)
+        quantize_dec(0)
+        decode(1, 0, 6)
+        decode(0, 0, 3)
+        tanh_late(0)
+        cast_dec(1, nc.vector.tensor_copy)
+        encode(3, 0)
         quantize_dec(1)
-        cast_dec(2)
-        scale_h(1, 0)
-        finish(2, 0, 6)
+        subtract(1, 0)
+        subtract(0, 0)
+        park(0, 1)
+        tanh_late(1)
+        encode(2, 4)
+        park(1, 1)
+        tanh_late(3)
+        tanh_late(2)
         scale_h(1, 1)
-        finish(3, 0, 7)
-        quantize_dec(2)
+        square(0, 0)
+        cast_dec(2, nc.scalar.copy)
+        scale_h(1, 0)
+        decode(3, 0, 6)
         quantize_h(1, 0)
+        park(3, 1)
         quantize_h(1, 1)
-        late_y(2, 2)
-        finish(4, 0, 6)
-        late_y(3, 3)
-        finish(5, 0, 7)
-        late_y(4, 4)
-        finish(0, 1, 0)
-        late_y(5, 5)
-        for n in range(1, N_TILES):
-            finish(n, 1, (0, 1, 6, 7, 2, 3)[n])
+        decode(0, 1, 2)
+        decode(1, 1, 5)
+        subtract(3, 0)
+        decode(2, 0, 1)
+        late_y(4, 0, 0)
+        subtract(2, 0)
+        late_y(4, 1, 7)
+        late_y(5, 0, 3)
+        park(5, 0)
+        late_y(5, 1, 1)
+        square(2, 0)
+        park(4, 1)
+        subtract(1, 1)
+        park(5, 1)
+        park(4, 0)
+        quantize_dec(2)
+        decode(4, 1, 7)
+        decode(4, 0, 0)
+        decode(5, 0, 6)
+        decode(3, 1, 3)
+        decode(2, 1, 4)
+        subtract(4, 0)
+        subtract(5, 0)
+        decode(5, 1, 1)
+        subtract(2, 1)
+        square(4, 0)
+        subtract(0, 1)
+        subtract(3, 1)
+        square(2, 1)
+        square(1, 0)
+        subtract(5, 1)
+        square(1, 1)
+        square(3, 0)
+        square(3, 1)
+        square(0, 1)
+        square(5, 0)
+        square(5, 1)
+        subtract(4, 1, pieces=2)
+        square(4, 1, pieces=2)

@@ -24,9 +24,10 @@ HALF = 512
 HALVES = S // HALF
 N_TILES = N // P
 WORD_BYTES = 512 * T
-ENC_SCALAR_SHARE = ((32,), (0,), (72,), (16, 24))
-Y_SLOT = {(1, 1): 'enc_raw31', (3, 1): 'enc_raw20', (0, 1): 'enc_raw00', (2, 1): 'enc_raw30'}
-ENC_PIECES = (1, 1, 1, 2)
+ENC_SCALAR_SHARE = ((56,), (16,), (56,), (48,))
+Y_SLOT = {(3, 1): 'enc_raw20', (2, 1): 'enc_bf3', (1, 1): 'enc_raw30', (0, 1): 'enc_bf0'}
+DEC_LOADS = ((0, 256), (256, 768))
+ENC_PIECES = (1, 1, 1, 1)
 DEC_CHUNK = 256
 H_CHUNK = 256
 TILE_WORDS = 2 * P // 4
@@ -67,8 +68,6 @@ def tile_list_alarm_anomaly_maps_kernel(tc, tab, offs, enc, b, gain, dec, tgt_wo
             for c in range(ENC_PIECES[a])
         }
         dec_raw = held("dec_raw", [P, PACK, N], F32)
-        b_sb = held("b_sb", [P, PACK], F32)
-        gain_sb = held("gain_sb", [P, PACK], F32)
         tgt_rows = tgt_words.bitcast(I32).rearrange("a p c -> p a c")
 
         def load_words(m):
@@ -96,8 +95,10 @@ def tile_list_alarm_anomaly_maps_kernel(tc, tab, offs, enc, b, gain, dec, tgt_wo
 
         load_tgt(0)
         load_words(1)
-        nc.gpsimd.dma_start(b_sb[:], b.rearrange("(p t) -> p t", t=PACK))
-        nc.gpsimd.dma_start(gain_sb[:], gain.rearrange("(p t) -> p t", t=PACK))
+        channel = held("channel", [P, 2, 8], F32, tag="picked_sc")
+        b_sb, gain_sb = channel[:, 0, :PACK], channel[:, 1, :PACK]
+        nc.scalar.dma_start(b_sb, b.rearrange("(p t) -> p t", t=PACK))
+        nc.scalar.dma_start(gain_sb, gain.rearrange("(p t) -> p t", t=PACK))
         load_tgt(1)
         for a in range(PASSES):
             rows = enc[512 * a : 512 * (a + 1), :].rearrange("(p j) c -> p j c", j=PACK)
@@ -105,15 +106,15 @@ def tile_list_alarm_anomaly_maps_kernel(tc, tab, offs, enc, b, gain, dec, tgt_wo
             for c in range(ENC_PIECES[a]):
                 nc.sync.dma_start(enc_raw[a, c][:], rows[:, :, c * width : (c + 1) * width])
         dec_rows = dec.rearrange("(p j) c -> p j c", j=PACK)
-        for c in range(0, N, DEC_CHUNK):
-            nc.sync.dma_start(dec_raw[:, :, c : c + DEC_CHUNK], dec_rows[:, :, c : c + DEC_CHUNK])
-            if c == 1 * DEC_CHUNK:
+        for i, (c0, c1) in enumerate(DEC_LOADS):
+            nc.sync.dma_start(dec_raw[:, :, c0:c1], dec_rows[:, :, c0:c1])
+            if i == min(0, len(DEC_LOADS) - 1):
                 nc.sync.dma_start(tgt_last[:], tgt_rows[:, :, EARLY_TILES * TILE_WORDS :])
 
         v_words = {}
 
         def gather(m, u):
-            picked = held("picked", [P, HALF], I32)
+            picked = held(f"picked{m}{u}", [P, HALF], I32, tag="picked")
             cols = slice(u * HALF // 16, (u + 1) * HALF // 16)
             nc.vector.tensor_copy(picked[:].bitcast(U32), words[m][:].bitcast(U32).indirect(offsets[:, cols]))
             parted = held(f"parted{m}{u}", [P, 2, HALF], U16)
@@ -174,9 +175,15 @@ def tile_list_alarm_anomaly_maps_kernel(tc, tab, offs, enc, b, gain, dec, tgt_wo
                 src = enc_raw[a, c][:].rearrange("p j (m t) -> p m t j", t=PACK)
                 cut = width - ENC_SCALAR_SHARE[a][c]
                 if cut > 0:
-                    nc.vector.tensor_copy(dst[:, c * width : c * width + cut], src[:, :cut])
+                    nc.vector.tensor_copy(
+                        dst[:, c * width : c * width + cut].rearrange("p m (s e) j -> p s m j e", e=2),
+                        src[:, :cut].rearrange("p m (s e) j -> p s m j e", e=2),
+                    )
                 if cut < width:
-                    nc.scalar.copy(dst[:, c * width + cut : (c + 1) * width], src[:, cut:])
+                    nc.scalar.copy(
+                        dst[:, c * width + cut : (c + 1) * width].rearrange("p m (s e) j -> p s m j e", e=2),
+                        src[:, cut:].rearrange("p m (s e) j -> p s m j e", e=2),
+                    )
             codes = held(f"enc_codes{a}", [P, H], U32)
             scales = held(f"enc_scales{a}", [P, H], U8)
             nc.vector.quantize_mx(out=codes[:].bitcast(FP8X4), scales=scales[:], in_=grouped[:])
@@ -246,7 +253,7 @@ def tile_list_alarm_anomaly_maps_kernel(tc, tab, offs, enc, b, gain, dec, tgt_wo
         h_codes = [held(f"h_codes{u}", [P, HALF], U32) for u in range(HALVES)]
         h_scales = [held(f"h_scales{u}", [P, HALF], U8) for u in range(HALVES)]
         h_bf = [held(f"h_bf{u}", [P, PACK * HALF], BF16) for u in range(HALVES)]
-        gains = gain_sb[:].rearrange("p (c t i) -> p c t i", c=1, i=1).to_broadcast([P, H_CHUNK // 4, PACK, 4])
+        gains = gain_sb.rearrange("p (c t i) -> p c t i", c=1, i=1).to_broadcast([P, H_CHUNK // 4, PACK, 4])
 
         def scale_h(u, c):
             wide = slice(c * H_CHUNK * PACK, (c + 1) * H_CHUNK * PACK)
@@ -296,73 +303,73 @@ def tile_list_alarm_anomaly_maps_kernel(tc, tab, offs, enc, b, gain, dec, tgt_wo
                     nc.scalar.activation(res[:, cols], diff[:, cols], ACT.Square)
                 nc.sync.dma_start(out[P * n : P * (n + 1), u * HALF + c : u * HALF + c + width], res[:, cols])
 
-        encode(1, 1)
-        park(2, 1)
-        scale_h(0, 0)
         scale_h(0, 1)
-        quantize_h(0, 0)
-        cast_dec(0, nc.vector.tensor_copy)
-        quantize_h(0, 1)
-        encode(0, 0)
-        quantize_dec(0)
-        decode(1, 0, 6)
-        decode(0, 0, 3)
-        tanh_late(0)
-        cast_dec(1, nc.vector.tensor_copy)
-        encode(3, 0)
-        quantize_dec(1)
-        subtract(1, 0)
-        subtract(0, 0)
         park(0, 1)
-        tanh_late(1)
+        cast_dec(0, nc.vector.tensor_copy)
+        encode(3, 2)
+        encode(0, 0)
+        scale_h(0, 0)
+        quantize_h(0, 0)
+        quantize_h(0, 1)
         encode(2, 4)
+        park(2, 1)
+        cast_dec(1, nc.scalar.copy)
+        quantize_dec(0)
+        quantize_dec(1)
+        park(3, 1)
+        decode(1, 0, 6)
         park(1, 1)
         tanh_late(3)
-        tanh_late(2)
-        scale_h(1, 1)
-        square(0, 0)
         cast_dec(2, nc.scalar.copy)
-        scale_h(1, 0)
-        decode(3, 0, 6)
-        quantize_h(1, 0)
-        park(3, 1)
-        quantize_h(1, 1)
-        decode(0, 1, 2)
-        decode(1, 1, 5)
-        subtract(3, 0)
-        decode(2, 0, 1)
-        late_y(4, 0, 0)
-        subtract(2, 0)
-        late_y(4, 1, 7)
-        late_y(5, 0, 3)
-        park(5, 0)
-        late_y(5, 1, 1)
-        square(2, 0)
-        park(4, 1)
-        subtract(1, 1)
-        park(5, 1)
-        park(4, 0)
+        tanh_late(2)
+        encode(1, 1)
         quantize_dec(2)
-        decode(4, 1, 7)
-        decode(4, 0, 0)
-        decode(5, 0, 6)
-        decode(3, 1, 3)
-        decode(2, 1, 4)
-        subtract(4, 0)
-        subtract(5, 0)
-        decode(5, 1, 1)
-        subtract(2, 1)
-        square(4, 0)
-        subtract(0, 1)
+        tanh_late(1)
+        tanh_late(0)
+        decode(2, 0, 4)
+        subtract(1, 0)
+        scale_h(1, 0)
+        scale_h(1, 1)
+        quantize_h(1, 1)
+        decode(3, 0, 7)
+        quantize_h(1, 0)
+        late_y(4, 0, 5)
+        decode(0, 0, 3)
+        decode(4, 0, 1)
+        subtract(0, 0)
+        park(4, 0)
+        late_y(4, 1, 2)
+        subtract(2, 0)
+        square(2, 0)
+        late_y(5, 1, 6)
+        decode(1, 1, 0)
+        late_y(5, 0, 5)
+        square(0, 0)
+        park(5, 0)
+        subtract(3, 0, pieces=2)
+        park(4, 1)
+        decode(0, 1, 7)
+        decode(3, 1, 2)
         subtract(3, 1)
-        square(2, 1)
-        square(1, 0)
-        subtract(5, 1)
-        square(1, 1)
-        square(3, 0)
-        square(3, 1)
+        subtract(1, 1)
+        subtract(0, 1)
+        decode(4, 1, 4)
         square(0, 1)
-        square(5, 0)
+        square(1, 0)
+        decode(2, 1, 3)
+        subtract(2, 1)
+        decode(5, 1, 3)
+        subtract(4, 0)
+        park(5, 1)
+        subtract(5, 1)
         square(5, 1)
-        subtract(4, 1, pieces=2)
-        square(4, 1, pieces=2)
+        subtract(4, 1)
+        decode(5, 0, 1)
+        square(4, 0)
+        subtract(5, 0)
+        square(2, 1)
+        square(1, 1)
+        square(3, 1)
+        square(4, 1)
+        square(5, 0)
+        square(3, 0, pieces=2)

@@ -17,21 +17,21 @@ ACT = mybir.ActivationFunctionType
 ALU = mybir.AluOpType
 
 P = 128
+QUAD = 32
 PACK = 4
-PASSES = K // (P * PACK)
+K_PASS = P * PACK
+PASSES = K // K_PASS
 PAIRS = PASSES // 2
+WORD_BYTES = P * T * 4
 HALF = 512
 HALVES = S // HALF
 N_TILES = N // P
-WORD_BYTES = 512 * T
-ENC_SCALAR_SHARE = ((56,), (16,), (56,), (48,))
-Y_SLOT = {(3, 1): 'enc_raw20', (2, 1): 'enc_bf3', (1, 1): 'enc_raw30', (0, 1): 'enc_bf0'}
-DEC_LOADS = ((0, 256), (256, 768))
-ENC_PIECES = (1, 1, 1, 1)
-DEC_CHUNK = 256
+TILE_I32 = 2 * P // 4
+EARLY = 4
 H_CHUNK = 256
-TILE_WORDS = 2 * P // 4
-EARLY_TILES = 4
+DEC_CHUNK = 256
+DEC_FIRST = 512
+ENC_SCALAR_SHARE = (48, 16, 48, 64)
 
 
 def tile_list_alarm_anomaly_maps_kernel(tc, tab, offs, enc, b, gain, dec, tgt_words, tgt_scales, out):
@@ -43,73 +43,60 @@ def tile_list_alarm_anomaly_maps_kernel(tc, tab, offs, enc, b, gain, dec, tgt_wo
         def held(name, shape, dtype, tag=None):
             return keep.tile(shape, dtype, name=name, tag=tag or name, align_bytes=64)
 
-        def bank(i):
-            return psum.tile([P, HALF], F32, name=f"bank{i}", tag=f"bank{i}")
+        def bank(bk):
+            return psum.tile([P, HALF], F32, name=f"bank{bk}", tag=f"bank{bk}")
 
         offsets = keep.tile([P, S // 16], U16, name="offsets")
         nc.sync.dma_start(offsets[:], offs)
 
         scale_rows = held("scale_rows", [P, T // 4], I32)
         tgt_sc = held("tgt_sc", [P, PASSES, N // 4], I32)
-        v_sc = held("v_sc", [P, PASSES, S // 4], I32)
-        warm = held("warm", [P, 8], F32)
         nc.vector.memset(tgt_sc[:], 0)
-        nc.vector.memset(scale_rows[0:32, :], 0)
-        nc.vector.memset(scale_rows[96:P, :], 0)
-        nc.vector.memset(v_sc[:], 0)
-        nc.vector.memset(warm[:], 0.0)
+        nc.vector.memset(scale_rows[:QUAD, :], 0)
+        nc.vector.memset(scale_rows[3 * QUAD :, :], 0)
 
         words = [held(f"words{m}", [P, T], I32) for m in range(PAIRS)]
-        tgt_w = [held(f"tgt_w{m}", [P, 2, EARLY_TILES * TILE_WORDS], I32) for m in range(PAIRS)]
-        tgt_last = held("tgt_last", [P, PASSES, (N_TILES - EARLY_TILES) * TILE_WORDS], I32)
-        enc_raw = {
-            (a, c): held(f"enc_raw{a}{c}", [P, PACK, H // ENC_PIECES[a]], F32)
-            for a in range(PASSES)
-            for c in range(ENC_PIECES[a])
-        }
+        tgt_early = [held(f"tgt_early{m}", [P, 2, EARLY * TILE_I32], I32) for m in range(PAIRS)]
+        tgt_late = held("tgt_late", [P, PASSES, (N_TILES - EARLY) * TILE_I32], I32)
+        enc_raw = [held(f"enc_raw{a}", [P, PACK, H], F32) for a in range(PASSES)]
         dec_raw = held("dec_raw", [P, PACK, N], F32)
         tgt_rows = tgt_words.bitcast(I32).rearrange("a p c -> p a c")
 
         def load_words(m):
-            nc.sync.dma_start(words[m][:], tab[m, :WORD_BYTES].bitcast(I32).rearrange("(p t) -> p t", p=P))
+            nc.sync.dma_start(words[m][:], tab[m, :WORD_BYTES].bitcast(I32).rearrange("(p c) -> p c", p=P))
 
-        def load_tgt(m):
-            nc.sync.dma_start(tgt_w[m][:], tgt_rows[:, 2 * m : 2 * m + 2, : EARLY_TILES * TILE_WORDS])
+        def load_tgt_early(m):
+            nc.sync.dma_start(tgt_early[m][:], tgt_rows[:, 2 * m : 2 * m + 2, : EARLY * TILE_I32])
 
         for m in range(PAIRS):
-            rows = tab[m, WORD_BYTES:].bitcast(I32).rearrange("(h q t) -> q h t", h=2, q=16)
-            nc.sync.dma_start(scale_rows[32 + m : 96 : 2, :], rows)
-        for q in range(4):
-            nc.sync.dma_start(
-                tgt_sc[32 * q : 32 * q + 4, :, :],
-                tgt_scales[:, 4 * q : 4 * q + 4, :].bitcast(I32).rearrange("a r c -> r a c"),
-            )
+            rows = tab[m, WORD_BYTES:].bitcast(I32).rearrange("(e g c) -> g e c", e=2, g=16)
+            nc.sync.dma_start(scale_rows[QUAD + m : 3 * QUAD : 2, :], rows)
+        tgt_scale_rows = tgt_scales.bitcast(I32).rearrange("a (q row) c -> row q a c", row=4)
+        for row in range(4):
+            nc.sync.dma_start(tgt_sc[row:P:QUAD, :, :], tgt_scale_rows[row])
         load_words(0)
-        nc.scalar.activation(warm[:], warm[:], ACT.Tanh)
+        load_tgt_early(0)
 
         picked_sc = held("picked_sc", [P, S // 4], I32)
         nc.vector.tensor_copy(picked_sc[:].bitcast(U8), scale_rows[:].bitcast(U8).indirect(offsets[:]))
-        for q in range(4):
-            nc.sync.dma_start(v_sc[32 * q : 32 * q + 4, :, :], picked_sc[32 + 16 * q : 48 + 16 * q, :])
+        v_sc = held("v_sc", [P, PASSES, S // 4], I32, tag="scale_rows")
+        for q in (0, 2, 1, 3):
+            nc.sync.dma_start(v_sc[QUAD * q : QUAD * q + 4, :, :], picked_sc[QUAD + 16 * q : QUAD + 16 * (q + 1), :])
         v_scales = [v_sc[:, 2 * (a % 2) + a // 2, :].bitcast(U8) for a in range(PASSES)]
 
-        load_tgt(0)
         load_words(1)
         channel = held("channel", [P, 2, 8], F32, tag="picked_sc")
         b_sb, gain_sb = channel[:, 0, :PACK], channel[:, 1, :PACK]
         nc.scalar.dma_start(b_sb, b.rearrange("(p t) -> p t", t=PACK))
         nc.scalar.dma_start(gain_sb, gain.rearrange("(p t) -> p t", t=PACK))
-        load_tgt(1)
+        load_tgt_early(1)
         for a in range(PASSES):
-            rows = enc[512 * a : 512 * (a + 1), :].rearrange("(p j) c -> p j c", j=PACK)
-            width = H // ENC_PIECES[a]
-            for c in range(ENC_PIECES[a]):
-                nc.sync.dma_start(enc_raw[a, c][:], rows[:, :, c * width : (c + 1) * width])
-        dec_rows = dec.rearrange("(p j) c -> p j c", j=PACK)
-        for i, (c0, c1) in enumerate(DEC_LOADS):
-            nc.sync.dma_start(dec_raw[:, :, c0:c1], dec_rows[:, :, c0:c1])
-            if i == min(0, len(DEC_LOADS) - 1):
-                nc.sync.dma_start(tgt_last[:], tgt_rows[:, :, EARLY_TILES * TILE_WORDS :])
+            rows = enc[K_PASS * a : K_PASS * (a + 1), :].rearrange("(p w) c -> p w c", w=PACK)
+            nc.sync.dma_start(enc_raw[a][:], rows)
+        dec_rows = dec.rearrange("(p t) c -> p t c", t=PACK)
+        nc.sync.dma_start(dec_raw[:, :, :DEC_FIRST], dec_rows[:, :, :DEC_FIRST])
+        nc.sync.dma_start(tgt_late[:], tgt_rows[:, :, EARLY * TILE_I32 :])
+        nc.sync.dma_start(dec_raw[:, :, DEC_FIRST:], dec_rows[:, :, DEC_FIRST:])
 
         v_words = {}
 
@@ -118,118 +105,102 @@ def tile_list_alarm_anomaly_maps_kernel(tc, tab, offs, enc, b, gain, dec, tgt_wo
             cols = slice(u * HALF // 16, (u + 1) * HALF // 16)
             nc.vector.tensor_copy(picked[:].bitcast(U32), words[m][:].bitcast(U32).indirect(offsets[:, cols]))
             parted = held(f"parted{m}{u}", [P, 2, HALF], U16)
-            nc.vector.tensor_copy(parted[:], picked[:].bitcast(U16).rearrange("p (s h) -> p h s", h=2))
-            for h in range(2):
-                v_words[2 * m + h, u] = parted[:, h, :].bitcast(FP4X4)
+            nc.vector.tensor_copy(
+                parted[:].rearrange("p e (port j) -> p port e j", port=2),
+                picked[:].bitcast(U16).rearrange("p (port j e) -> p port e j", port=2, e=2),
+            )
+            for e in range(2):
+                v_words[2 * m + e, u] = parted[:, e, :].bitcast(FP4X4)
 
-        def v_operand(a, u):
-            return dict(rhs=v_words[a, u], rhs_scale=v_scales[a][:, u * HALF : (u + 1) * HALF])
-
-        def y_pass(acc, n, u, a):
-            if n < EARLY_TILES:
-                codes = tgt_w[a // 2][:, a % 2, TILE_WORDS * n : TILE_WORDS * (n + 1)]
-            else:
-                codes = tgt_last[:, a, TILE_WORDS * (n - EARLY_TILES) : TILE_WORDS * (n - EARLY_TILES + 1)]
+        def times_v(acc, codes, scales, a, u):
             nc.tensor.matmul_mx(
                 out=acc[:],
-                lhsT=codes.bitcast(FP4X4),
-                lhsT_scale=tgt_sc[:, a, 32 * n : 32 * (n + 1)].bitcast(U8),
+                lhsT=codes,
+                lhsT_scale=scales,
+                rhs=v_words[a, u],
+                rhs_scale=v_scales[a][:, u * HALF : (u + 1) * HALF],
                 start=(a == 0),
                 stop=(a == PASSES - 1),
-                **v_operand(a, u),
             )
 
-        y_sb = {}
-
-        def keep_y(acc, n, u):
-            y_sb[n, u] = held(f"y{n}{u}", [P, HALF], F32, tag=Y_SLOT.get((n, u)))
-            nc.scalar.copy(y_sb[n, u][:], acc[:])
-
         y_acc = {}
+        y_sb = {}
+        y_buffer = {(2, 1): f"enc_raw{PASSES - 1}", (3, 1): f"enc_bf{PASSES - 1}"}
 
-        def late_y(n, u, i):
-            y_acc[n, u] = bank(i)
-            for a in range(PASSES):
-                y_pass(y_acc[n, u], n, u, a)
+        def y_pass(n, u, a):
+            if n < EARLY:
+                codes = tgt_early[a // 2][:, a % 2, TILE_I32 * n : TILE_I32 * (n + 1)]
+            else:
+                codes = tgt_late[:, a, TILE_I32 * (n - EARLY) : TILE_I32 * (n - EARLY + 1)]
+            scales = tgt_sc[:, a, P // 4 * n : P // 4 * (n + 1)]
+            times_v(y_acc[n, u], codes.bitcast(FP4X4), scales.bitcast(U8), a, u)
 
         def park(n, u):
-            keep_y(y_acc[n, u] if n >= EARLY_TILES else accs[EARLY_TILES + n], n, u)
+            y_sb[n, u] = held(f"y{n}{u}", [P, HALF], F32, tag=y_buffer.get((n, u)))
+            nc.scalar.copy(y_sb[n, u][:], y_acc[n, u][:])
 
-        first = [(n, 0) for n in range(EARLY_TILES)] + [(n, 1) for n in range(8 - EARLY_TILES)]
-        accs = [bank(i) for i in range(8)]
+        def late_y(n, u, bk):
+            y_acc[n, u] = bank(bk)
+            for a in range(PASSES):
+                y_pass(n, u, a)
+            park(n, u)
+
+        for u in range(HALVES):
+            for n in range(EARLY):
+                y_acc[n, u] = bank(EARLY * u + n)
         for u in range(HALVES):
             gather(0, u)
             for a in (0, 1):
-                for i, (n, uu) in enumerate(first):
-                    if uu == u:
-                        y_pass(accs[i], n, u, a)
+                for n in range(EARLY):
+                    y_pass(n, u, a)
         for u in range(HALVES):
             gather(1, u)
 
         enc_q = []
         for a in range(PASSES):
             grouped = held(f"enc_bf{a}", [P, PACK * H], BF16)
-            dst = grouped[:].rearrange("p (t m j) -> p m t j", t=PACK, j=PACK)
-            width = P // ENC_PIECES[a]
-            for c in range(ENC_PIECES[a]):
-                src = enc_raw[a, c][:].rearrange("p j (m t) -> p m t j", t=PACK)
-                cut = width - ENC_SCALAR_SHARE[a][c]
-                if cut > 0:
-                    nc.vector.tensor_copy(
-                        dst[:, c * width : c * width + cut].rearrange("p m (s e) j -> p s m j e", e=2),
-                        src[:, :cut].rearrange("p m (s e) j -> p s m j e", e=2),
-                    )
-                if cut < width:
-                    nc.scalar.copy(
-                        dst[:, c * width + cut : (c + 1) * width].rearrange("p m (s e) j -> p s m j e", e=2),
-                        src[:, cut:].rearrange("p m (s e) j -> p s m j e", e=2),
-                    )
+            dst = grouped[:].rearrange("p (hi lo o w) -> p hi o w lo", hi=2, lo=2, w=PACK)
+            src = enc_raw[a][:].rearrange("p w (o hi lo) -> p hi o w lo", hi=2, lo=2)
+            cut = P - ENC_SCALAR_SHARE[a]
+            nc.vector.tensor_copy(dst[:, :, :cut], src[:, :, :cut])
+            nc.scalar.copy(dst[:, :, cut:], src[:, :, cut:])
             codes = held(f"enc_codes{a}", [P, H], U32)
             scales = held(f"enc_scales{a}", [P, H], U8)
             nc.vector.quantize_mx(out=codes[:].bitcast(FP8X4), scales=scales[:], in_=grouped[:])
             enc_q.append((codes, scales))
 
         for u in range(HALVES):
-            for i, (n, uu) in enumerate(first):
-                if uu == u:
-                    for a in (2, 3):
-                        y_pass(accs[i], n, u, a)
-                    if u == 0:
-                        keep_y(accs[i], n, u)
+            for n in range(EARLY):
+                for a in (2, 3):
+                    y_pass(n, u, a)
+                if u == 0:
+                    park(n, u)
 
-        a_acc = {}
+        z_acc = {}
         th = [held(f"th{u}", [P, PACK, HALF], F32) for u in range(HALVES)]
+        chunks = [slice(start, start + H_CHUNK) for start in range(0, HALF, H_CHUNK)]
 
-        def a_pass(a, u, t):
+        def z_pass(a, u, t):
             codes, scales = enc_q[a]
-            nc.tensor.matmul_mx(
-                out=a_acc[u, t][:],
-                lhsT=codes[:, P * t : P * (t + 1)].bitcast(FP8X4),
-                lhsT_scale=scales[:, P * t : P * (t + 1)],
-                start=(a == 0),
-                stop=(a == PASSES - 1),
-                **v_operand(a, u),
-            )
+            cols = slice(P * t, P * (t + 1))
+            times_v(z_acc[u, t], codes[:, cols].bitcast(FP8X4), scales[:, cols], a, u)
 
         def tanh(u, t, cols):
-            nc.scalar.activation(th[u][:, t, cols], a_acc[u, t][:, cols], ACT.Tanh, bias=b_sb[:, t : t + 1])
+            nc.scalar.activation(th[u][:, t, cols], z_acc[u, t][:, cols], ACT.Tanh, bias=b_sb[:, t : t + 1])
 
-        chunks = [slice(c * H_CHUNK, (c + 1) * H_CHUNK) for c in range(HALF // H_CHUNK)]
         for t in range(PACK):
-            a_acc[0, t] = bank(t)
+            z_acc[0, t] = bank(t)
         for a in range(PASSES):
             for t in range(PACK):
-                a_pass(a, 0, t)
+                z_pass(a, 0, t)
         for cols in chunks:
             for t in range(PACK):
                 tanh(0, t, cols)
 
-        def encode(t, i):
-            a_acc[1, t] = bank(i)
+        def encode_second_half(t, bk):
+            z_acc[1, t] = bank(bk)
             for a in range(PASSES):
-                a_pass(a, 1, t)
-
-        def tanh_late(t):
+                z_pass(a, 1, t)
             for cols in chunks if t == PACK - 1 else [slice(0, HALF)]:
                 tanh(1, t, cols)
 
@@ -237,44 +208,36 @@ def tile_list_alarm_anomaly_maps_kernel(tc, tab, offs, enc, b, gain, dec, tgt_wo
         dec_codes = held("dec_codes", [P, N], U32)
         dec_scales = held("dec_scales", [P, N], U8)
 
-        def cast_dec(c, copy):
-            cols = slice(c * DEC_CHUNK, (c + 1) * DEC_CHUNK)
-            wide = slice(c * DEC_CHUNK * PACK, (c + 1) * DEC_CHUNK * PACK)
+        def quantize_dec(start, copy):
+            cols = slice(start, start + DEC_CHUNK)
+            grouped = dec_bf[:, PACK * cols.start : PACK * cols.stop]
             copy(
-                dec_bf[:, wide].rearrange("p (c i t) -> p c t i", i=4, t=PACK),
+                grouped.rearrange("p (c i t) -> p c t i", i=4, t=PACK),
                 dec_raw[:, :, cols].rearrange("p t (c i) -> p c t i", i=4),
             )
-
-        def quantize_dec(c):
-            cols = slice(c * DEC_CHUNK, (c + 1) * DEC_CHUNK)
-            wide = slice(c * DEC_CHUNK * PACK, (c + 1) * DEC_CHUNK * PACK)
-            nc.vector.quantize_mx(out=dec_codes[:, cols].bitcast(FP8X4), scales=dec_scales[:, cols], in_=dec_bf[:, wide])
+            nc.vector.quantize_mx(out=dec_codes[:, cols].bitcast(FP8X4), scales=dec_scales[:, cols], in_=grouped)
 
         h_codes = [held(f"h_codes{u}", [P, HALF], U32) for u in range(HALVES)]
         h_scales = [held(f"h_scales{u}", [P, HALF], U8) for u in range(HALVES)]
         h_bf = [held(f"h_bf{u}", [P, PACK * HALF], BF16) for u in range(HALVES)]
         gains = gain_sb.rearrange("p (c t i) -> p c t i", c=1, i=1).to_broadcast([P, H_CHUNK // 4, PACK, 4])
 
-        def scale_h(u, c):
-            wide = slice(c * H_CHUNK * PACK, (c + 1) * H_CHUNK * PACK)
-            nc.vector.tensor_tensor(
-                h_bf[u][:, wide].rearrange("p (c i t) -> p c t i", i=4, t=PACK),
-                th[u][:, :, chunks[c]].rearrange("p t (c i) -> p c t i", i=4),
-                gains,
-                ALU.mult,
-            )
+        def quantize_h(u):
+            grouped = [h_bf[u][:, PACK * cols.start : PACK * cols.stop] for cols in chunks]
+            for cols, dst in zip(chunks, grouped):
+                nc.vector.tensor_tensor(
+                    dst.rearrange("p (c i t) -> p c t i", i=4, t=PACK),
+                    th[u][:, :, cols].rearrange("p t (c i) -> p c t i", i=4),
+                    gains,
+                    ALU.mult,
+                )
+            for cols, src in zip(chunks, grouped):
+                nc.vector.quantize_mx(out=h_codes[u][:, cols].bitcast(FP8X4), scales=h_scales[u][:, cols], in_=src)
 
-        def quantize_h(u, c):
-            wide = slice(c * H_CHUNK * PACK, (c + 1) * H_CHUNK * PACK)
-            nc.vector.quantize_mx(
-                out=h_codes[u][:, chunks[c]].bitcast(FP8X4), scales=h_scales[u][:, chunks[c]], in_=h_bf[u][:, wide]
-            )
-
-        d_acc = {}
         diffs = {}
 
-        def decode(n, u, i):
-            d = d_acc[n, u] = bank(i)
+        def residual(n, u, bk, parts):
+            d = bank(bk)
             nc.tensor.matmul_mx(
                 out=d[:],
                 lhsT=dec_codes[:, P * n : P * (n + 1)].bitcast(FP8X4),
@@ -284,92 +247,36 @@ def tile_list_alarm_anomaly_maps_kernel(tc, tab, offs, enc, b, gain, dec, tgt_wo
                 start=True,
                 stop=True,
             )
-
-        def subtract(n, u, pieces=1):
             diffs[n, u] = held(f"diff{n}{u}", [P, HALF], F32)
-            width = HALF // pieces
-            for c in range(0, HALF, width):
-                cols = slice(c, c + width)
-                nc.vector.tensor_tensor(diffs[n, u][:, cols], y_sb[n, u][:, cols], d_acc[n, u][:, cols], ALU.subtract)
+            for cols in parts:
+                nc.vector.tensor_tensor(diffs[n, u][:, cols], y_sb[n, u][:, cols], d[:, cols], ALU.subtract)
 
-        def square(n, u, on_gpsimd=False, pieces=1):
-            diff, res = diffs[n, u], y_sb[n, u]
-            width = HALF // pieces
-            for c in range(0, HALF, width):
-                cols = slice(c, c + width)
-                if on_gpsimd:
-                    nc.gpsimd.tensor_tensor(res[:, cols], diff[:, cols], diff[:, cols], ALU.mult)
-                else:
-                    nc.scalar.activation(res[:, cols], diff[:, cols], ACT.Square)
-                nc.sync.dma_start(out[P * n : P * (n + 1), u * HALF + c : u * HALF + c + width], res[:, cols])
+        def square(n, u, parts):
+            rows = out[P * n : P * (n + 1), u * HALF : (u + 1) * HALF]
+            for cols in parts:
+                nc.scalar.activation(y_sb[n, u][:, cols], diffs[n, u][:, cols], ACT.Square)
+                nc.sync.dma_start(rows[:, cols], y_sb[n, u][:, cols])
 
-        scale_h(0, 1)
-        park(0, 1)
-        cast_dec(0, nc.vector.tensor_copy)
-        encode(3, 2)
-        encode(0, 0)
-        scale_h(0, 0)
-        quantize_h(0, 0)
-        quantize_h(0, 1)
-        encode(2, 4)
-        park(2, 1)
-        cast_dec(1, nc.scalar.copy)
-        quantize_dec(0)
-        quantize_dec(1)
-        park(3, 1)
-        decode(1, 0, 6)
-        park(1, 1)
-        tanh_late(3)
-        cast_dec(2, nc.scalar.copy)
-        tanh_late(2)
-        encode(1, 1)
-        quantize_dec(2)
-        tanh_late(1)
-        tanh_late(0)
-        decode(2, 0, 4)
-        subtract(1, 0)
-        scale_h(1, 0)
-        scale_h(1, 1)
-        quantize_h(1, 1)
-        decode(3, 0, 7)
-        quantize_h(1, 0)
+        whole = [slice(0, HALF)]
+        for n in range(EARLY):
+            park(n, 1)
+        for start in range(0, DEC_FIRST, DEC_CHUNK):
+            quantize_dec(start, nc.vector.tensor_copy)
+        quantize_h(0)
+        quantize_dec(DEC_FIRST, nc.scalar.copy)
+        for n, bk in enumerate((6, 7, 3)):
+            residual(n, 0, bk, whole)
+        for t, bk in enumerate((4, 0, 1, 2)):
+            encode_second_half(t, bk)
+        residual(3, 0, 4, whole)
+        quantize_h(1)
         late_y(4, 0, 5)
-        decode(0, 0, 3)
-        decode(4, 0, 1)
-        subtract(0, 0)
-        park(4, 0)
-        late_y(4, 1, 2)
-        subtract(2, 0)
-        square(2, 0)
-        late_y(5, 1, 6)
-        decode(1, 1, 0)
-        late_y(5, 0, 5)
-        square(0, 0)
-        park(5, 0)
-        subtract(3, 0, pieces=2)
-        park(4, 1)
-        decode(0, 1, 7)
-        decode(3, 1, 2)
-        subtract(3, 1)
-        subtract(1, 1)
-        subtract(0, 1)
-        decode(4, 1, 4)
-        square(0, 1)
-        square(1, 0)
-        decode(2, 1, 3)
-        subtract(2, 1)
-        decode(5, 1, 3)
-        subtract(4, 0)
-        park(5, 1)
-        subtract(5, 1)
-        square(5, 1)
-        subtract(4, 1)
-        decode(5, 0, 1)
-        square(4, 0)
-        subtract(5, 0)
-        square(2, 1)
-        square(1, 1)
-        square(3, 1)
-        square(4, 1)
-        square(5, 0)
-        square(3, 0, pieces=2)
+        for n in range(EARLY):
+            square(n, 0, whole)
+        for (n, u), bk in zip(((5, 0), (4, 1), (5, 1)), (5, 0, 1)):
+            late_y(n, u, bk)
+        rest = [(n, 0) for n in range(EARLY, N_TILES)] + [(n, 1) for n in range(N_TILES)]
+        for (n, u), bk in zip(rest, (6, 7, 3, 4, 2, 6, 7, 3)):
+            parts = chunks if (n, u) == rest[-1] else whole
+            residual(n, u, bk, parts)
+            square(n, u, parts)

@@ -31,7 +31,7 @@ EARLY = 4
 H_CHUNK = 256
 DEC_CHUNK = 256
 DEC_FIRST = 512
-ENC_SCALAR_SHARE = (48, 16, 48, 64)
+ENC_SCALAR_SHARE = (64, 32, 0, 80)
 
 
 def tile_list_alarm_anomaly_maps_kernel(tc, tab, offs, enc, b, gain, dec, tgt_words, tgt_scales, out):
@@ -50,10 +50,12 @@ def tile_list_alarm_anomaly_maps_kernel(tc, tab, offs, enc, b, gain, dec, tgt_wo
         nc.sync.dma_start(offsets[:], offs)
 
         scale_rows = held("scale_rows", [P, T // 4], I32)
-        tgt_sc = held("tgt_sc", [P, PASSES, N // 4], I32)
+        tgt_sc = held("tgt_sc", [P, PASSES, EARLY * P // 4], I32)
+        tgt_sc_late = held("tgt_sc_late", [P, PASSES, (N_TILES - EARLY) * P // 4], I32)
         nc.vector.memset(tgt_sc[:], 0)
         nc.vector.memset(scale_rows[:QUAD, :], 0)
         nc.vector.memset(scale_rows[3 * QUAD :, :], 0)
+        nc.vector.memset(tgt_sc_late[:], 0)
 
         words = [held(f"words{m}", [P, T], I32) for m in range(PAIRS)]
         tgt_early = [held(f"tgt_early{m}", [P, 2, EARLY * TILE_I32], I32) for m in range(PAIRS)]
@@ -73,18 +75,24 @@ def tile_list_alarm_anomaly_maps_kernel(tc, tab, offs, enc, b, gain, dec, tgt_wo
             nc.sync.dma_start(scale_rows[QUAD + m : 3 * QUAD : 2, :], rows)
         tgt_scale_rows = tgt_scales.bitcast(I32).rearrange("a (q row) c -> row q a c", row=4)
         for row in range(4):
-            nc.sync.dma_start(tgt_sc[row:P:QUAD, :, :], tgt_scale_rows[row])
+            nc.sync.dma_start(tgt_sc[row:P:QUAD, :, :], tgt_scale_rows[row][:, :, : EARLY * P // 4])
         load_words(0)
-        load_tgt_early(0)
 
         picked_sc = held("picked_sc", [P, S // 4], I32)
         nc.vector.tensor_copy(picked_sc[:].bitcast(U8), scale_rows[:].bitcast(U8).indirect(offsets[:]))
         v_sc = held("v_sc", [P, PASSES, S // 4], I32, tag="scale_rows")
-        for q in (0, 2, 1, 3):
-            nc.sync.dma_start(v_sc[QUAD * q : QUAD * q + 4, :, :], picked_sc[QUAD + 16 * q : QUAD + 16 * (q + 1), :])
-        v_scales = [v_sc[:, 2 * (a % 2) + a // 2, :].bitcast(U8) for a in range(PASSES)]
 
+        def move_scales(m):
+            for q in (0, 2, 1, 3):
+                rows = picked_sc[QUAD + 16 * q + m : QUAD + 16 * (q + 1) : 2, :]
+                nc.sync.dma_start(v_sc[QUAD * q : QUAD * q + 4, 2 * m : 2 * m + 2, :], rows)
+
+        v_scales = [v_sc[:, a, :].bitcast(U8) for a in range(PASSES)]
+
+        move_scales(0)
+        load_tgt_early(0)
         load_words(1)
+        move_scales(1)
         channel = held("channel", [P, 2, 8], F32, tag="picked_sc")
         b_sb, gain_sb = channel[:, 0, :PACK], channel[:, 1, :PACK]
         nc.scalar.dma_start(b_sb, b.rearrange("(p t) -> p t", t=PACK))
@@ -94,46 +102,54 @@ def tile_list_alarm_anomaly_maps_kernel(tc, tab, offs, enc, b, gain, dec, tgt_wo
             rows = enc[K_PASS * a : K_PASS * (a + 1), :].rearrange("(p w) c -> p w c", w=PACK)
             nc.sync.dma_start(enc_raw[a][:], rows)
         dec_rows = dec.rearrange("(p t) c -> p t c", t=PACK)
-        nc.sync.dma_start(dec_raw[:, :, :DEC_FIRST], dec_rows[:, :, :DEC_FIRST])
+        for start in range(0, DEC_FIRST, DEC_CHUNK):
+            nc.sync.dma_start(dec_raw[:, :, start : start + DEC_CHUNK], dec_rows[:, :, start : start + DEC_CHUNK])
         nc.sync.dma_start(tgt_late[:], tgt_rows[:, :, EARLY * TILE_I32 :])
+        for row in range(4):
+            nc.sync.dma_start(tgt_sc_late[row:P:QUAD, :, :], tgt_scale_rows[row][:, :, EARLY * P // 4 :])
         nc.sync.dma_start(dec_raw[:, :, DEC_FIRST:], dec_rows[:, :, DEC_FIRST:])
 
         v_words = {}
 
-        def gather(m, u):
+        def gather(m, u, parts):
+            parted = held(f"parted{m}{u}", [P, 2, HALF], U16)
             picked = held(f"picked{m}{u}", [P, HALF], I32, tag="picked")
             cols = slice(u * HALF // 16, (u + 1) * HALF // 16)
             nc.vector.tensor_copy(picked[:].bitcast(U32), words[m][:].bitcast(U32).indirect(offsets[:, cols]))
-            parted = held(f"parted{m}{u}", [P, 2, HALF], U16)
-            nc.vector.tensor_copy(
-                parted[:].rearrange("p e (port j) -> p port e j", port=2),
-                picked[:].bitcast(U16).rearrange("p (port j e) -> p port e j", port=2, e=2),
-            )
+            for part in parts:
+                nc.vector.tensor_copy(
+                    parted[:, :, part].rearrange("p e (port j) -> p port e j", port=2),
+                    picked[:, part].bitcast(U16).rearrange("p (port j e) -> p port e j", port=2, e=2),
+                )
             for e in range(2):
-                v_words[2 * m + e, u] = parted[:, e, :].bitcast(FP4X4)
+                v_words[2 * m + e, u] = parted[:, e, :]
 
-        def times_v(acc, codes, scales, a, u):
+        def times_v(acc, codes, scales, a, u, part):
             nc.tensor.matmul_mx(
-                out=acc[:],
+                out=acc[:, part],
                 lhsT=codes,
                 lhsT_scale=scales,
-                rhs=v_words[a, u],
-                rhs_scale=v_scales[a][:, u * HALF : (u + 1) * HALF],
-                start=(a == 0),
-                stop=(a == PASSES - 1),
+                rhs=v_words[a, u][:, part].bitcast(FP4X4),
+                rhs_scale=v_scales[a][:, u * HALF + part.start : u * HALF + part.stop],
+                start=(a == 0 and part.start == 0),
+                stop=(a == PASSES - 1 and part.stop == HALF),
             )
+
+        whole = [slice(0, HALF)]
+        chunks = [slice(start, start + H_CHUNK) for start in range(0, HALF, H_CHUNK)]
 
         y_acc = {}
         y_sb = {}
-        y_buffer = {(2, 1): f"enc_raw{PASSES - 1}", (3, 1): f"enc_bf{PASSES - 1}"}
+        y_buffer = {}
 
-        def y_pass(n, u, a):
+        def y_pass(n, u, a, part=whole[0]):
             if n < EARLY:
                 codes = tgt_early[a // 2][:, a % 2, TILE_I32 * n : TILE_I32 * (n + 1)]
+                scales = tgt_sc[:, a, P // 4 * n : P // 4 * (n + 1)]
             else:
                 codes = tgt_late[:, a, TILE_I32 * (n - EARLY) : TILE_I32 * (n - EARLY + 1)]
-            scales = tgt_sc[:, a, P // 4 * n : P // 4 * (n + 1)]
-            times_v(y_acc[n, u], codes.bitcast(FP4X4), scales.bitcast(U8), a, u)
+                scales = tgt_sc_late[:, a, P // 4 * (n - EARLY) : P // 4 * (n - EARLY + 1)]
+            times_v(y_acc[n, u], codes.bitcast(FP4X4), scales.bitcast(U8), a, u, part)
 
         def park(n, u):
             y_sb[n, u] = held(f"y{n}{u}", [P, HALF], F32, tag=y_buffer.get((n, u)))
@@ -149,12 +165,14 @@ def tile_list_alarm_anomaly_maps_kernel(tc, tab, offs, enc, b, gain, dec, tgt_wo
             for n in range(EARLY):
                 y_acc[n, u] = bank(EARLY * u + n)
         for u in range(HALVES):
-            gather(0, u)
-            for a in (0, 1):
-                for n in range(EARLY):
-                    y_pass(n, u, a)
+            parts = chunks if u == 0 else whole
+            gather(0, u, parts)
+            for part in parts:
+                for a in (0, 1):
+                    for n in range(EARLY):
+                        y_pass(n, u, a, part)
         for u in range(HALVES):
-            gather(1, u)
+            gather(1, u, chunks if u == 0 else whole)
 
         enc_q = []
         for a in range(PASSES):
@@ -162,28 +180,44 @@ def tile_list_alarm_anomaly_maps_kernel(tc, tab, offs, enc, b, gain, dec, tgt_wo
             dst = grouped[:].rearrange("p (hi lo o w) -> p hi o w lo", hi=2, lo=2, w=PACK)
             src = enc_raw[a][:].rearrange("p w (o hi lo) -> p hi o w lo", hi=2, lo=2)
             cut = P - ENC_SCALAR_SHARE[a]
-            nc.vector.tensor_copy(dst[:, :, :cut], src[:, :, :cut])
-            nc.scalar.copy(dst[:, :, cut:], src[:, :, cut:])
             codes = held(f"enc_codes{a}", [P, H], U32)
             scales = held(f"enc_scales{a}", [P, H], U8)
-            nc.vector.quantize_mx(out=codes[:].bitcast(FP8X4), scales=scales[:], in_=grouped[:])
+            if a < PASSES - 1:
+                nc.vector.tensor_copy(dst[:, :, :cut], src[:, :, :cut])
+                if cut < P:
+                    nc.scalar.copy(dst[:, :, cut:], src[:, :, cut:])
+                nc.vector.quantize_mx(out=codes[:].bitcast(FP8X4), scales=scales[:], in_=grouped[:])
+            else:
+                nc.vector.tensor_copy(dst[:, 0], src[:, 0])
+                nc.scalar.copy(dst[:, 1, cut:], src[:, 1, cut:])
+                nc.vector.tensor_copy(dst[:, 1, :cut], src[:, 1, :cut])
+                for hi in range(2):
+                    cols = slice(hi * H // 2, (hi + 1) * H // 2)
+                    nc.vector.quantize_mx(
+                        out=codes[:, cols].bitcast(FP8X4),
+                        scales=scales[:, cols],
+                        in_=grouped[:, PACK * cols.start : PACK * cols.stop],
+                    )
             enc_q.append((codes, scales))
 
-        for u in range(HALVES):
+        for part in chunks:
             for n in range(EARLY):
                 for a in (2, 3):
-                    y_pass(n, u, a)
-                if u == 0:
-                    park(n, u)
+                    y_pass(n, 0, a, part)
+        for n in range(EARLY):
+            park(n, 0)
+        for n in range(EARLY):
+            for a in (2, 3):
+                y_pass(n, 1, a)
+            park(n, 1)
 
         z_acc = {}
         th = [held(f"th{u}", [P, PACK, HALF], F32) for u in range(HALVES)]
-        chunks = [slice(start, start + H_CHUNK) for start in range(0, HALF, H_CHUNK)]
 
         def z_pass(a, u, t):
             codes, scales = enc_q[a]
             cols = slice(P * t, P * (t + 1))
-            times_v(z_acc[u, t], codes[:, cols].bitcast(FP8X4), scales[:, cols], a, u)
+            times_v(z_acc[u, t], codes[:, cols].bitcast(FP8X4), scales[:, cols], a, u, whole[0])
 
         def tanh(u, t, cols):
             nc.scalar.activation(th[u][:, t, cols], z_acc[u, t][:, cols], ACT.Tanh, bias=b_sb[:, t : t + 1])
@@ -224,7 +258,16 @@ def tile_list_alarm_anomaly_maps_kernel(tc, tab, offs, enc, b, gain, dec, tgt_wo
 
         def quantize_h(u):
             grouped = [h_bf[u][:, PACK * cols.start : PACK * cols.stop] for cols in chunks]
-            for cols, dst in zip(chunks, grouped):
+            if u == 1:
+                rows = held("h_rows", [P, PACK, HALF], BF16)
+                for t in range(PACK):
+                    nc.gpsimd.tensor_scalar(rows[:, t, :], th[u][:, t, :], gain_sb[:, t : t + 1], 0.0, ALU.mult, ALU.add)
+                for cols, dst in zip(chunks, grouped):
+                    nc.vector.tensor_copy(
+                        dst.rearrange("p (c i t) -> p c t i", i=4, t=PACK),
+                        rows[:, :, cols].rearrange("p t (c i) -> p c t i", i=4),
+                    )
+            for cols, dst in zip(chunks, grouped) if u == 0 else []:
                 nc.vector.tensor_tensor(
                     dst.rearrange("p (c i t) -> p c t i", i=4, t=PACK),
                     th[u][:, :, cols].rearrange("p t (c i) -> p c t i", i=4),
@@ -257,12 +300,9 @@ def tile_list_alarm_anomaly_maps_kernel(tc, tab, offs, enc, b, gain, dec, tgt_wo
                 nc.scalar.activation(y_sb[n, u][:, cols], diffs[n, u][:, cols], ACT.Square)
                 nc.sync.dma_start(rows[:, cols], y_sb[n, u][:, cols])
 
-        whole = [slice(0, HALF)]
-        for n in range(EARLY):
-            park(n, 1)
-        for start in range(0, DEC_FIRST, DEC_CHUNK):
-            quantize_dec(start, nc.vector.tensor_copy)
+        quantize_dec(0, nc.vector.tensor_copy)
         quantize_h(0)
+        quantize_dec(DEC_CHUNK, nc.vector.tensor_copy)
         quantize_dec(DEC_FIRST, nc.scalar.copy)
         for n, bk in enumerate((6, 7, 3)):
             residual(n, 0, bk, whole)
@@ -270,13 +310,11 @@ def tile_list_alarm_anomaly_maps_kernel(tc, tab, offs, enc, b, gain, dec, tgt_wo
             encode_second_half(t, bk)
         residual(3, 0, 4, whole)
         quantize_h(1)
-        late_y(4, 0, 5)
-        for n in range(EARLY):
-            square(n, 0, whole)
-        for (n, u), bk in zip(((5, 0), (4, 1), (5, 1)), (5, 0, 1)):
-            late_y(n, u, bk)
-        rest = [(n, 0) for n in range(EARLY, N_TILES)] + [(n, 1) for n in range(N_TILES)]
-        for (n, u), bk in zip(rest, (6, 7, 3, 4, 2, 6, 7, 3)):
-            parts = chunks if (n, u) == rest[-1] else whole
-            residual(n, u, bk, parts)
-            square(n, u, parts)
+        for n, bk in enumerate((6, 7, 3, 4)):
+            residual(n, 1, bk, whole)
+        for (n, u), y_bank, d_bank in (((4, 0), 5, 5), ((5, 0), 0, 6), ((4, 1), 1, 7), ((5, 1), 2, 3)):
+            late_y(n, u, y_bank)
+            residual(n, u, d_bank, chunks if (n, u) == (5, 1) else whole)
+        for n, u in [(n, 0) for n in range(EARLY)] + [(4, 0), (0, 1), (1, 1), (5, 0), (2, 1), (3, 1), (4, 1)]:
+            square(n, u, whole)
+        square(5, 1, chunks)

@@ -32,6 +32,7 @@ H_CHUNK = 256
 DEC_CHUNK = 256
 DEC_FIRST = 512
 ENC_SCALAR_SHARE = (64, 32, 0, 80)
+POOL_COLUMNS = 192
 
 
 def tile_list_alarm_anomaly_maps_kernel(tc, tab, offs, enc, b, gain, dec, tgt_words, tgt_scales, out):
@@ -77,6 +78,7 @@ def tile_list_alarm_anomaly_maps_kernel(tc, tab, offs, enc, b, gain, dec, tgt_wo
         for row in range(4):
             nc.sync.dma_start(tgt_sc[row:P:QUAD, :, :], tgt_scale_rows[row][:, :, : EARLY * P // 4])
         load_words(0)
+        load_tgt_early(0)
 
         picked_sc = held("picked_sc", [P, S // 4], I32)
         nc.vector.tensor_copy(picked_sc[:].bitcast(U8), scale_rows[:].bitcast(U8).indirect(offsets[:]))
@@ -90,7 +92,6 @@ def tile_list_alarm_anomaly_maps_kernel(tc, tab, offs, enc, b, gain, dec, tgt_wo
         v_scales = [v_sc[:, a, :].bitcast(U8) for a in range(PASSES)]
 
         move_scales(0)
-        load_tgt_early(0)
         load_words(1)
         move_scales(1)
         channel = held("channel", [P, 2, 8], F32, tag="picked_sc")
@@ -140,7 +141,6 @@ def tile_list_alarm_anomaly_maps_kernel(tc, tab, offs, enc, b, gain, dec, tgt_wo
 
         y_acc = {}
         y_sb = {}
-        y_buffer = {}
 
         def y_pass(n, u, a, part=whole[0]):
             if n < EARLY:
@@ -152,7 +152,7 @@ def tile_list_alarm_anomaly_maps_kernel(tc, tab, offs, enc, b, gain, dec, tgt_wo
             times_v(y_acc[n, u], codes.bitcast(FP4X4), scales.bitcast(U8), a, u, part)
 
         def park(n, u):
-            y_sb[n, u] = held(f"y{n}{u}", [P, HALF], F32, tag=y_buffer.get((n, u)))
+            y_sb[n, u] = held(f"y{n}{u}", [P, HALF], F32)
             nc.scalar.copy(y_sb[n, u][:], y_acc[n, u][:])
 
         def late_y(n, u, bk):
@@ -256,26 +256,27 @@ def tile_list_alarm_anomaly_maps_kernel(tc, tab, offs, enc, b, gain, dec, tgt_wo
         h_bf = [held(f"h_bf{u}", [P, PACK * HALF], BF16) for u in range(HALVES)]
         gains = gain_sb.rearrange("p (c t i) -> p c t i", c=1, i=1).to_broadcast([P, H_CHUNK // 4, PACK, 4])
 
+        def interleaved(u, cols):
+            return h_bf[u][:, PACK * cols.start : PACK * cols.stop].rearrange("p (c i t) -> p c t i", i=4, t=PACK)
+
         def quantize_h(u):
-            grouped = [h_bf[u][:, PACK * cols.start : PACK * cols.stop] for cols in chunks]
-            if u == 1:
-                rows = held("h_rows", [P, PACK, HALF], BF16)
-                for t in range(PACK):
-                    nc.gpsimd.tensor_scalar(rows[:, t, :], th[u][:, t, :], gain_sb[:, t : t + 1], 0.0, ALU.mult, ALU.add)
-                for cols, dst in zip(chunks, grouped):
-                    nc.vector.tensor_copy(
-                        dst.rearrange("p (c i t) -> p c t i", i=4, t=PACK),
-                        rows[:, :, cols].rearrange("p t (c i) -> p c t i", i=4),
-                    )
-            for cols, dst in zip(chunks, grouped) if u == 0 else []:
-                nc.vector.tensor_tensor(
-                    dst.rearrange("p (c i t) -> p c t i", i=4, t=PACK),
-                    th[u][:, :, cols].rearrange("p t (c i) -> p c t i", i=4),
-                    gains,
-                    ALU.mult,
-                )
-            for cols, src in zip(chunks, grouped):
-                nc.vector.quantize_mx(out=h_codes[u][:, cols].bitcast(FP8X4), scales=h_scales[u][:, cols], in_=src)
+            for cols in chunks:
+                grouped = h_bf[u][:, PACK * cols.start : PACK * cols.stop]
+                nc.vector.quantize_mx(out=h_codes[u][:, cols].bitcast(FP8X4), scales=h_scales[u][:, cols], in_=grouped)
+
+        def first_h():
+            for cols in chunks:
+                rows = th[0][:, :, cols].rearrange("p t (c i) -> p c t i", i=4)
+                nc.vector.tensor_tensor(interleaved(0, cols), rows, gains, ALU.mult)
+            quantize_h(0)
+
+        def second_h():
+            rows = held("h_rows", [P, PACK, HALF], BF16)
+            for t in range(PACK):
+                nc.gpsimd.tensor_scalar(rows[:, t, :], th[1][:, t, :], gain_sb[:, t : t + 1], 0.0, ALU.mult, ALU.add)
+            for cols in chunks:
+                nc.vector.tensor_copy(interleaved(1, cols), rows[:, :, cols].rearrange("p t (c i) -> p c t i", i=4))
+            quantize_h(1)
 
         diffs = {}
 
@@ -294,14 +295,18 @@ def tile_list_alarm_anomaly_maps_kernel(tc, tab, offs, enc, b, gain, dec, tgt_wo
             for cols in parts:
                 nc.vector.tensor_tensor(diffs[n, u][:, cols], y_sb[n, u][:, cols], d[:, cols], ALU.subtract)
 
-        def square(n, u, parts):
+        def square(n, u, parts, shared=0):
             rows = out[P * n : P * (n + 1), u * HALF : (u + 1) * HALF]
             for cols in parts:
-                nc.scalar.activation(y_sb[n, u][:, cols], diffs[n, u][:, cols], ACT.Square)
+                cut = cols.stop - shared
+                nc.scalar.activation(y_sb[n, u][:, cols.start : cut], diffs[n, u][:, cols.start : cut], ACT.Square)
+                if shared:
+                    rest = diffs[n, u][:, cut : cols.stop]
+                    nc.gpsimd.tensor_tensor(y_sb[n, u][:, cut : cols.stop], rest, rest, ALU.mult)
                 nc.sync.dma_start(rows[:, cols], y_sb[n, u][:, cols])
 
         quantize_dec(0, nc.vector.tensor_copy)
-        quantize_h(0)
+        first_h()
         quantize_dec(DEC_CHUNK, nc.vector.tensor_copy)
         quantize_dec(DEC_FIRST, nc.scalar.copy)
         for n, bk in enumerate((6, 7, 3)):
@@ -309,12 +314,14 @@ def tile_list_alarm_anomaly_maps_kernel(tc, tab, offs, enc, b, gain, dec, tgt_wo
         for t, bk in enumerate((4, 0, 1, 2)):
             encode_second_half(t, bk)
         residual(3, 0, 4, whole)
-        quantize_h(1)
+        second_h()
         for n, bk in enumerate((6, 7, 3, 4)):
             residual(n, 1, bk, whole)
         for (n, u), y_bank, d_bank in (((4, 0), 5, 5), ((5, 0), 0, 6), ((4, 1), 1, 7), ((5, 1), 2, 3)):
             late_y(n, u, y_bank)
             residual(n, u, d_bank, chunks if (n, u) == (5, 1) else whole)
-        for n, u in [(n, 0) for n in range(EARLY)] + [(4, 0), (0, 1), (1, 1), (5, 0), (2, 1), (3, 1), (4, 1)]:
-            square(n, u, whole)
+        for n in range(EARLY):
+            square(n, 0, whole)
+        for n, u in [(4, 0), (0, 1), (1, 1), (5, 0), (2, 1), (3, 1), (4, 1)]:
+            square(n, u, whole, POOL_COLUMNS)
         square(5, 1, chunks)

@@ -103,12 +103,11 @@ def tile_list_alarm_anomaly_maps_kernel(tc, tab, offs, enc, b, gain, dec, tgt_wo
             rows = enc[K_PASS * a : K_PASS * (a + 1), :].rearrange("(p w) c -> p w c", w=PACK)
             nc.sync.dma_start(enc_raw[a][:], rows)
         dec_rows = dec.rearrange("(p t) c -> p t c", t=PACK)
-        for start in range(0, DEC_FIRST, DEC_CHUNK):
+        for start in range(0, N, DEC_CHUNK):
             nc.sync.dma_start(dec_raw[:, :, start : start + DEC_CHUNK], dec_rows[:, :, start : start + DEC_CHUNK])
         nc.sync.dma_start(tgt_late[:], tgt_rows[:, :, EARLY * TILE_I32 :])
         for row in range(4):
             nc.sync.dma_start(tgt_sc_late[row:P:QUAD, :, :], tgt_scale_rows[row][:, :, EARLY * P // 4 :])
-        nc.sync.dma_start(dec_raw[:, :, DEC_FIRST:], dec_rows[:, :, DEC_FIRST:])
 
         v_words = {}
 

@@ -68,8 +68,8 @@ def tile_list_alarm_anomaly_maps_kernel(tc, tab, offs, enc, b, gain, dec, tgt_wo
         def load_words(m):
             nc.sync.dma_start(words[m][:], tab[m, :WORD_BYTES].bitcast(I32).rearrange("(p c) -> p c", p=P))
 
-        def load_tgt_early(m):
-            nc.sync.dma_start(tgt_early[m][:], tgt_rows[:, 2 * m : 2 * m + 2, : EARLY * TILE_I32])
+        def load_tgt_early(m, e):
+            nc.sync.dma_start(tgt_early[m][:, e, :], tgt_rows[:, 2 * m + e.start : 2 * m + e.stop, : EARLY * TILE_I32])
 
         for m in range(PAIRS):
             rows = tab[m, WORD_BYTES:].bitcast(I32).rearrange("(e g c) -> g e c", e=2, g=16)
@@ -78,7 +78,7 @@ def tile_list_alarm_anomaly_maps_kernel(tc, tab, offs, enc, b, gain, dec, tgt_wo
         for row in range(4):
             nc.sync.dma_start(tgt_sc[row:P:QUAD, :, :], tgt_scale_rows[row][:, :, : EARLY * P // 4])
         load_words(0)
-        load_tgt_early(0)
+        load_tgt_early(0, slice(0, 2))
 
         picked_sc = held("picked_sc", [P, S // 4], I32)
         nc.vector.tensor_copy(picked_sc[:].bitcast(U8), scale_rows[:].bitcast(U8).indirect(offsets[:]))
@@ -98,7 +98,7 @@ def tile_list_alarm_anomaly_maps_kernel(tc, tab, offs, enc, b, gain, dec, tgt_wo
         b_sb, gain_sb = channel[:, 0, :PACK], channel[:, 1, :PACK]
         nc.scalar.dma_start(b_sb, b.rearrange("(p t) -> p t", t=PACK))
         nc.scalar.dma_start(gain_sb, gain.rearrange("(p t) -> p t", t=PACK))
-        load_tgt_early(1)
+        load_tgt_early(1, slice(0, 2))
         for a in range(PASSES):
             rows = enc[K_PASS * a : K_PASS * (a + 1), :].rearrange("(p w) c -> p w c", w=PACK)
             nc.sync.dma_start(enc_raw[a][:], rows)
@@ -111,16 +111,19 @@ def tile_list_alarm_anomaly_maps_kernel(tc, tab, offs, enc, b, gain, dec, tgt_wo
 
         v_words = {}
 
-        def gather(m, u, parts):
+        def gather(m, u, parts, picks):
             parted = held(f"parted{m}{u}", [P, 2, HALF], U16)
-            picked = held(f"picked{m}{u}", [P, HALF], I32, tag="picked")
-            cols = slice(u * HALF // 16, (u + 1) * HALF // 16)
-            nc.vector.tensor_copy(picked[:].bitcast(U32), words[m][:].bitcast(U32).indirect(offsets[:, cols]))
-            for part in parts:
-                nc.vector.tensor_copy(
-                    parted[:, :, part].rearrange("p e (port j) -> p port e j", port=2),
-                    picked[:, part].bitcast(U16).rearrange("p (port j e) -> p port e j", port=2, e=2),
-                )
+            for pick in picks:
+                picked = held(f"picked{m}{u}{pick.start}", [P, HALF], I32, tag="picked")
+                cols = slice((u * HALF + pick.start) // 16, (u * HALF + pick.stop) // 16)
+                window = words[m][:].bitcast(U32).indirect(offsets[:, cols])
+                nc.vector.tensor_copy(picked[:, pick].bitcast(U32), window)
+                for part in parts:
+                    if pick.start <= part.start < pick.stop:
+                        nc.vector.tensor_copy(
+                            parted[:, :, part].rearrange("p e (port j) -> p port e j", port=2),
+                            picked[:, part].bitcast(U16).rearrange("p (port j e) -> p port e j", port=2, e=2),
+                        )
             for e in range(2):
                 v_words[2 * m + e, u] = parted[:, e, :]
 
@@ -165,13 +168,13 @@ def tile_list_alarm_anomaly_maps_kernel(tc, tab, offs, enc, b, gain, dec, tgt_wo
                 y_acc[n, u] = bank(EARLY * u + n)
         for u in range(HALVES):
             parts = chunks if u == 0 else whole
-            gather(0, u, parts)
+            gather(0, u, parts, parts)
             for part in parts:
                 for a in (0, 1):
                     for n in range(EARLY):
                         y_pass(n, u, a, part)
         for u in range(HALVES):
-            gather(1, u, chunks if u == 0 else whole)
+            gather(1, u, chunks if u == 0 else whole, whole)
 
         enc_q = []
         for a in range(PASSES):

@@ -30,8 +30,9 @@ TILE_I32 = 2 * P // 4
 EARLY = 4
 H_CHUNK = 256
 DEC_CHUNK = 256
-DEC_FIRST = 512
-ENC_SCALAR_SHARE = (64, 32, 0, 80)
+DEC_LAST = N - DEC_CHUNK
+ENC_SCALAR_SHARE = (64, 32, 48, 96)
+ENC_WHOLE = 2
 POOL_COLUMNS = 192
 
 
@@ -68,8 +69,8 @@ def tile_list_alarm_anomaly_maps_kernel(tc, tab, offs, enc, b, gain, dec, tgt_wo
         def load_words(m):
             nc.sync.dma_start(words[m][:], tab[m, :WORD_BYTES].bitcast(I32).rearrange("(p c) -> p c", p=P))
 
-        def load_tgt_early(m, e):
-            nc.sync.dma_start(tgt_early[m][:, e, :], tgt_rows[:, 2 * m + e.start : 2 * m + e.stop, : EARLY * TILE_I32])
+        def load_tgt_early(m):
+            nc.sync.dma_start(tgt_early[m][:], tgt_rows[:, 2 * m : 2 * m + 2, : EARLY * TILE_I32])
 
         for m in range(PAIRS):
             rows = tab[m, WORD_BYTES:].bitcast(I32).rearrange("(e g c) -> g e c", e=2, g=16)
@@ -78,7 +79,7 @@ def tile_list_alarm_anomaly_maps_kernel(tc, tab, offs, enc, b, gain, dec, tgt_wo
         for row in range(4):
             nc.sync.dma_start(tgt_sc[row:P:QUAD, :, :], tgt_scale_rows[row][:, :, : EARLY * P // 4])
         load_words(0)
-        load_tgt_early(0, slice(0, 2))
+        load_tgt_early(0)
 
         picked_sc = held("picked_sc", [P, S // 4], I32)
         nc.vector.tensor_copy(picked_sc[:].bitcast(U8), scale_rows[:].bitcast(U8).indirect(offsets[:]))
@@ -98,7 +99,7 @@ def tile_list_alarm_anomaly_maps_kernel(tc, tab, offs, enc, b, gain, dec, tgt_wo
         b_sb, gain_sb = channel[:, 0, :PACK], channel[:, 1, :PACK]
         nc.scalar.dma_start(b_sb, b.rearrange("(p t) -> p t", t=PACK))
         nc.scalar.dma_start(gain_sb, gain.rearrange("(p t) -> p t", t=PACK))
-        load_tgt_early(1, slice(0, 2))
+        load_tgt_early(1)
         for a in range(PASSES):
             rows = enc[K_PASS * a : K_PASS * (a + 1), :].rearrange("(p w) c -> p w c", w=PACK)
             nc.sync.dma_start(enc_raw[a][:], rows)
@@ -184,10 +185,9 @@ def tile_list_alarm_anomaly_maps_kernel(tc, tab, offs, enc, b, gain, dec, tgt_wo
             cut = P - ENC_SCALAR_SHARE[a]
             codes = held(f"enc_codes{a}", [P, H], U32)
             scales = held(f"enc_scales{a}", [P, H], U8)
-            if a < PASSES - 1:
+            if a < ENC_WHOLE:
                 nc.vector.tensor_copy(dst[:, :, :cut], src[:, :, :cut])
-                if cut < P:
-                    nc.scalar.copy(dst[:, :, cut:], src[:, :, cut:])
+                nc.scalar.copy(dst[:, :, cut:], src[:, :, cut:])
                 nc.vector.quantize_mx(out=codes[:].bitcast(FP8X4), scales=scales[:], in_=grouped[:])
             else:
                 nc.vector.tensor_copy(dst[:, 0], src[:, 0])
@@ -310,7 +310,7 @@ def tile_list_alarm_anomaly_maps_kernel(tc, tab, offs, enc, b, gain, dec, tgt_wo
         quantize_dec(0, nc.vector.tensor_copy)
         first_h()
         quantize_dec(DEC_CHUNK, nc.vector.tensor_copy)
-        quantize_dec(DEC_FIRST, nc.scalar.copy)
+        quantize_dec(DEC_LAST, nc.scalar.copy)
         for n, bk in enumerate((6, 7, 3)):
             residual(n, 0, bk, whole)
         for t, bk in enumerate((4, 0, 1, 2)):

from contextlib import ExitStack

import concourse.mybir as mybir

K, T, S, H, N = 2048, 4096, 1024, 512, 768
FLOPS = 2 * S * (K * H + K * N + H * N)

F32 = mybir.dt.float32
BF16 = mybir.dt.bfloat16
I32 = mybir.dt.int32
U32 = mybir.dt.uint32
U16 = mybir.dt.uint16
U8 = mybir.dt.uint8
FP8X4 = mybir.dt.float8_e4m3fn_x4
FP4X4 = mybir.dt.float4_e2m1fn_x4
ACT = mybir.ActivationFunctionType
ALU = mybir.AluOpType

P = 128
QUAD = 32
PACK = 4
K_PASS = P * PACK
PASSES = K // K_PASS
PAIRS = PASSES // 2
WORD_BYTES = P * T * 4
HALF = 512
HALVES = S // HALF
N_TILES = N // P
TILE_I32 = 2 * P // 4
EARLY = 4
H_CHUNK = 256
DEC_CHUNK = 256
DEC_LAST = N - DEC_CHUNK
ENC_SCALAR_SHARE = (64, 32, 48, 96)
ENC_WHOLE = 2
POOL_COLUMNS = 192


def tile_list_alarm_anomaly_maps_kernel(tc, tab, offs, enc, b, gain, dec, tgt_words, tgt_scales, out):
    nc = tc.nc
    with ExitStack() as ctx:
        keep = ctx.enter_context(tc.tile_pool(name="keep", bufs=1))
        psum = ctx.enter_context(tc.psum_pool(name="psum", bufs=1))

        def held(name, shape, dtype, tag=None):
            return keep.tile(shape, dtype, name=name, tag=tag or name, align_bytes=64)

        def bank(bk):
            return psum.tile([P, HALF], F32, name=f"bank{bk}", tag=f"bank{bk}")

        offsets = keep.tile([P, S // 16], U16, name="offsets")
        nc.sync.dma_start(offsets[:], offs)

        scale_rows = held("scale_rows", [P, T // 4], I32)
        tgt_sc = held("tgt_sc", [P, PASSES, EARLY * P // 4], I32)
        tgt_sc_late = held("tgt_sc_late", [P, PASSES, (N_TILES - EARLY) * P // 4], I32)
        nc.vector.memset(tgt_sc[:], 0)
        nc.vector.memset(scale_rows[:QUAD, :], 0)
        nc.vector.memset(scale_rows[3 * QUAD :, :], 0)
        nc.vector.memset(tgt_sc_late[:], 0)

        words = [held(f"words{m}", [P, T], I32) for m in range(PAIRS)]
        tgt_early = [held(f"tgt_early{m}", [P, 2, EARLY * TILE_I32], I32) for m in range(PAIRS)]
        tgt_late = held("tgt_late", [P, PASSES, (N_TILES - EARLY) * TILE_I32], I32)
        enc_raw = [held(f"enc_raw{a}", [P, PACK, H], F32) for a in range(PASSES)]
        dec_raw = held("dec_raw", [P, PACK, N], F32)
        tgt_rows = tgt_words.bitcast(I32).rearrange("a p c -> p a c")

        def load_words(m):
            nc.sync.dma_start(words[m][:], tab[m, :WORD_BYTES].bitcast(I32).rearrange("(p c) -> p c", p=P))

        def load_tgt_early(m):
            nc.sync.dma_start(tgt_early[m][:], tgt_rows[:, 2 * m : 2 * m + 2, : EARLY * TILE_I32])

        for m in range(PAIRS):
            rows = tab[m, WORD_BYTES:].bitcast(I32).rearrange("(e g c) -> g e c", e=2, g=16)
            nc.sync.dma_start(scale_rows[QUAD + m : 3 * QUAD : 2, :], rows)
        tgt_scale_rows = tgt_scales.bitcast(I32).rearrange("a (q row) c -> row q a c", row=4)
        for row in range(4):
            nc.sync.dma_start(tgt_sc[row:P:QUAD, :, :], tgt_scale_rows[row][:, :, : EARLY * P // 4])
        load_words(0)
        load_tgt_early(0)

        picked_sc = held("picked_sc", [P, S // 4], I32)
        nc.vector.tensor_copy(picked_sc[:].bitcast(U8), scale_rows[:].bitcast(U8).indirect(offsets[:]))
        v_sc = held("v_sc", [P, PASSES, S // 4], I32, tag="scale_rows")

        def move_scales(m):
            for q in (0, 2, 1, 3):
                rows = picked_sc[QUAD + 16 * q + m : QUAD + 16 * (q + 1) : 2, :]
                nc.sync.dma_start(v_sc[QUAD * q : QUAD * q + 4, 2 * m : 2 * m + 2, :], rows)

        v_scales = [v_sc[:, a, :].bitcast(U8) for a in range(PASSES)]

        move_scales(0)
        load_words(1)
        move_scales(1)
        channel = held("channel", [P, 2, 8], F32, tag="picked_sc")
        b_sb, gain_sb = channel[:, 0, :PACK], channel[:, 1, :PACK]
        nc.scalar.dma_start(b_sb, b.rearrange("(p t) -> p t", t=PACK))
        nc.scalar.dma_start(gain_sb, gain.rearrange("(p t) -> p t", t=PACK))
        load_tgt_early(1)
        for a in range(PASSES):
            rows = enc[K_PASS * a : K_PASS * (a + 1), :].rearrange("(p w) c -> p w c", w=PACK)
            nc.sync.dma_start(enc_raw[a][:], rows)
        dec_rows = dec.rearrange("(p t) c -> p t c", t=PACK)
        for start in range(0, N, DEC_CHUNK):
            nc.sync.dma_start(dec_raw[:, :, start : start + DEC_CHUNK], dec_rows[:, :, start : start + DEC_CHUNK])
        nc.sync.dma_start(tgt_late[:], tgt_rows[:, :, EARLY * TILE_I32 :])
        for row in range(4):
            nc.sync.dma_start(tgt_sc_late[row:P:QUAD, :, :], tgt_scale_rows[row][:, :, EARLY * P // 4 :])

        v_words = {}

        def gather(m, u, parts, picks):
            parted = held(f"parted{m}{u}", [P, 2, HALF], U16)
            for pick in picks:
                picked = held(f"picked{m}{u}{pick.start}", [P, HALF], I32, tag="picked")
                cols = slice((u * HALF + pick.start) // 16, (u * HALF + pick.stop) // 16)
                window = words[m][:].bitcast(U32).indirect(offsets[:, cols])
                nc.vector.tensor_copy(picked[:, pick].bitcast(U32), window)
                for part in parts:
                    if pick.start <= part.start < pick.stop:
                        nc.vector.tensor_copy(
                            parted[:, :, part].rearrange("p e (port j) -> p port e j", port=2),
                            picked[:, part].bitcast(U16).rearrange("p (port j e) -> p port e j", port=2, e=2),
                        )
            for e in range(2):
                v_words[2 * m + e, u] = parted[:, e, :]

        def times_v(acc, codes, scales, a, u, part):
            nc.tensor.matmul_mx(
                out=acc[:, part],
                lhsT=codes,
                lhsT_scale=scales,
                rhs=v_words[a, u][:, part].bitcast(FP4X4),
                rhs_scale=v_scales[a][:, u * HALF + part.start : u * HALF + part.stop],
                start=(a == 0 and part.start == 0),
                stop=(a == PASSES - 1 and part.stop == HALF),
            )

        whole = [slice(0, HALF)]
        chunks = [slice(start, start + H_CHUNK) for start in range(0, HALF, H_CHUNK)]

        y_acc = {}
        y_sb = {}

        def y_pass(n, u, a, part=whole[0]):
            if n < EARLY:
                codes = tgt_early[a // 2][:, a % 2, TILE_I32 * n : TILE_I32 * (n + 1)]
                scales = tgt_sc[:, a, P // 4 * n : P // 4 * (n + 1)]
            else:
                codes = tgt_late[:, a, TILE_I32 * (n - EARLY) : TILE_I32 * (n - EARLY + 1)]
                scales = tgt_sc_late[:, a, P // 4 * (n - EARLY) : P // 4 * (n - EARLY + 1)]
            times_v(y_acc[n, u], codes.bitcast(FP4X4), scales.bitcast(U8), a, u, part)

        def park(n, u):
            y_sb[n, u] = held(f"y{n}{u}", [P, HALF], F32)
            nc.scalar.copy(y_sb[n, u][:], y_acc[n, u][:])

        def late_y(n, u, bk):
            y_acc[n, u] = bank(bk)
            for a in range(PASSES):
                y_pass(n, u, a)
            park(n, u)

        for u in range(HALVES):
            for n in range(EARLY):
                y_acc[n, u] = bank(EARLY * u + n)
        for u in range(HALVES):
            parts = chunks if u == 0 else whole
            gather(0, u, parts, parts)
            for part in parts:
                for a in (0, 1):
                    for n in range(EARLY):
                        y_pass(n, u, a, part)
        for u in range(HALVES):
            gather(1, u, chunks if u == 0 else whole, whole)

        enc_q = []
        for a in range(PASSES):
            grouped = held(f"enc_bf{a}", [P, PACK * H], BF16)
            dst = grouped[:].rearrange("p (hi lo o w) -> p hi o w lo", hi=2, lo=2, w=PACK)
            src = enc_raw[a][:].rearrange("p w (o hi lo) -> p hi o w lo", hi=2, lo=2)
            cut = P - ENC_SCALAR_SHARE[a]
            codes = held(f"enc_codes{a}", [P, H], U32)
            scales = held(f"enc_scales{a}", [P, H], U8)
            if a < ENC_WHOLE:
                nc.vector.tensor_copy(dst[:, :, :cut], src[:, :, :cut])
                nc.scalar.copy(dst[:, :, cut:], src[:, :, cut:])
                nc.vector.quantize_mx(out=codes[:].bitcast(FP8X4), scales=scales[:], in_=grouped[:])
            else:
                nc.vector.tensor_copy(dst[:, 0], src[:, 0])
                nc.scalar.copy(dst[:, 1, cut:], src[:, 1, cut:])
                nc.vector.tensor_copy(dst[:, 1, :cut], src[:, 1, :cut])
                for hi in range(2):
                    cols = slice(hi * H // 2, (hi + 1) * H // 2)
                    nc.vector.quantize_mx(
                        out=codes[:, cols].bitcast(FP8X4),
                        scales=scales[:, cols],
                        in_=grouped[:, PACK * cols.start : PACK * cols.stop],
                    )
            enc_q.append((codes, scales))

        for part in chunks:
            for n in range(EARLY):
                for a in (2, 3):
                    y_pass(n, 0, a, part)
        for n in range(EARLY):
            park(n, 0)
        for n in range(EARLY):
            for a in (2, 3):
                y_pass(n, 1, a)
            park(n, 1)

        z_acc = {}
        th = [held(f"th{u}", [P, PACK, HALF], F32) for u in range(HALVES)]

        def z_pass(a, u, t):
            codes, scales = enc_q[a]
            cols = slice(P * t, P * (t + 1))
            times_v(z_acc[u, t], codes[:, cols].bitcast(FP8X4), scales[:, cols], a, u, whole[0])

        def tanh(u, t, cols):
            nc.scalar.activation(th[u][:, t, cols], z_acc[u, t][:, cols], ACT.Tanh, bias=b_sb[:, t : t + 1])

        for t in range(PACK):
            z_acc[0, t] = bank(t)
        for a in range(PASSES):
            for t in range(PACK):
                z_pass(a, 0, t)
        for cols in chunks:
            for t in range(PACK):
                tanh(0, t, cols)

        def encode_second_half(t, bk):
            z_acc[1, t] = bank(bk)
            for a in range(PASSES):
                z_pass(a, 1, t)
            for cols in chunks if t == PACK - 1 else [slice(0, HALF)]:
                tanh(1, t, cols)

        dec_bf = held("dec_bf", [P, PACK * N], BF16)
        dec_codes = held("dec_codes", [P, N], U32)
        dec_scales = held("dec_scales", [P, N], U8)

        def quantize_dec(start, copy):
            cols = slice(start, start + DEC_CHUNK)
            grouped = dec_bf[:, PACK * cols.start : PACK * cols.stop]
            copy(
                grouped.rearrange("p (c i t) -> p c t i", i=4, t=PACK),
                dec_raw[:, :, cols].rearrange("p t (c i) -> p c t i", i=4),
            )
            nc.vector.quantize_mx(out=dec_codes[:, cols].bitcast(FP8X4), scales=dec_scales[:, cols], in_=grouped)

        h_codes = [held(f"h_codes{u}", [P, HALF], U32) for u in range(HALVES)]
        h_scales = [held(f"h_scales{u}", [P, HALF], U8) for u in range(HALVES)]
        h_bf = [held(f"h_bf{u}", [P, PACK * HALF], BF16) for u in range(HALVES)]
        gains = gain_sb.rearrange("p (c t i) -> p c t i", c=1, i=1).to_broadcast([P, H_CHUNK // 4, PACK, 4])

        def interleaved(u, cols):
            return h_bf[u][:, PACK * cols.start : PACK * cols.stop].rearrange("p (c i t) -> p c t i", i=4, t=PACK)

        def quantize_h(u):
            for cols in chunks:
                grouped = h_bf[u][:, PACK * cols.start : PACK * cols.stop]
                nc.vector.quantize_mx(out=h_codes[u][:, cols].bitcast(FP8X4), scales=h_scales[u][:, cols], in_=grouped)

        def first_h():
            for cols in chunks:
                rows = th[0][:, :, cols].rearrange("p t (c i) -> p c t i", i=4)
                nc.vector.tensor_tensor(interleaved(0, cols), rows, gains, ALU.mult)
            quantize_h(0)

        def second_h():
            rows = held("h_rows", [P, PACK, HALF], BF16)
            for t in range(PACK):
                nc.gpsimd.tensor_scalar(rows[:, t, :], th[1][:, t, :], gain_sb[:, t : t + 1], 0.0, ALU.mult, ALU.add)
            for cols in chunks:
                nc.vector.tensor_copy(interleaved(1, cols), rows[:, :, cols].rearrange("p t (c i) -> p c t i", i=4))
            quantize_h(1)

        diffs = {}

        def residual(n, u, bk, parts):
            d = bank(bk)
            nc.tensor.matmul_mx(
                out=d[:],
                lhsT=dec_codes[:, P * n : P * (n + 1)].bitcast(FP8X4),
                lhsT_scale=dec_scales[:, P * n : P * (n + 1)],
                rhs=h_codes[u][:].bitcast(FP8X4),
                rhs_scale=h_scales[u][:],
                start=True,
                stop=True,
            )
            diffs[n, u] = held(f"diff{n}{u}", [P, HALF], F32)
            for cols in parts:
                nc.vector.tensor_tensor(diffs[n, u][:, cols], y_sb[n, u][:, cols], d[:, cols], ALU.subtract)

        def square(n, u, parts, shared=0):
            rows = out[P * n : P * (n + 1), u * HALF : (u + 1) * HALF]
            for cols in parts:
                cut = cols.stop - shared
                nc.scalar.activation(y_sb[n, u][:, cols.start : cut], diffs[n, u][:, cols.start : cut], ACT.Square)
                if shared:
                    rest = diffs[n, u][:, cut : cols.stop]
                    nc.gpsimd.tensor_tensor(y_sb[n, u][:, cut : cols.stop], rest, rest, ALU.mult)
                nc.sync.dma_start(rows[:, cols], y_sb[n, u][:, cols])

        quantize_dec(0, nc.vector.tensor_copy)
        first_h()
        quantize_dec(DEC_CHUNK, nc.vector.tensor_copy)
        quantize_dec(DEC_LAST, nc.scalar.copy)
        for n, bk in enumerate((6, 7, 3)):
            residual(n, 0, bk, whole)
        for t, bk in enumerate((4, 0, 1, 2)):
            encode_second_half(t, bk)
        residual(3, 0, 4, whole)
        second_h()
        for n, bk in enumerate((6, 7, 3, 4)):
            residual(n, 1, bk, whole)
        for (n, u), y_bank, d_bank in (((4, 0), 5, 5), ((5, 0), 0, 6), ((4, 1), 1, 7), ((5, 1), 2, 3)):
            late_y(n, u, y_bank)
            residual(n, u, d_bank, chunks if (n, u) == (5, 1) else whole)
        for n in range(EARLY):
            square(n, 0, whole)
        for n, u in [(4, 0), (0, 1), (1, 1), (5, 0), (2, 1), (3, 1), (4, 1)]:
            square(n, u, whole, POOL_COLUMNS)
        square(5, 1, chunks)
